import numpy as np
import ml_dtypes


def mxq(x, axis, fmt="e4m3"):
    dtype, down = {"e4m3": (ml_dtypes.float8_e4m3fn, 7), "e5m2": (ml_dtypes.float8_e5m2, 14)}[fmt]
    v = np.moveaxis(np.asarray(x, np.float32).astype(ml_dtypes.bfloat16).astype(np.float64), axis, -1)
    blocks = v.reshape(v.shape[:-1] + (-1, 32))
    amax = np.abs(blocks).max(-1, keepdims=True)
    byte = np.maximum(np.where(amax > 0, np.frexp(amax)[1] - 1 + 127, 0) - down, 1)
    scale = np.exp2(byte - 127.0)
    codes = (blocks / scale).astype(np.float32).astype(dtype).astype(np.float64)
    return np.moveaxis((codes * scale).reshape(v.shape), -1, axis)


WIDE = False


def mx_kscale(k):
    if not WIDE:
        return np.ones(k)
    levels = np.array([24, -24, 12, -12, 0])
    if k % 512:
        return np.exp2(np.random.permutation(np.resize(levels, k // 32))).repeat(32)
    a = np.empty((k // 512, 16))
    for p in range(k // 512):
        a[p, :8] = np.random.permutation(np.resize(levels, 8))
        for g in range(8):
            far = levels[np.abs(levels - a[p, g]) >= 10]
            a[p, g + 8] = far[np.random.randint(len(far))]
    return np.exp2(a.ravel()).repeat(32)


def f64(x):
    return np.asarray(x).astype(np.float64)


def striped(idx):
    return np.tile(idx.reshape(-1, 16).T, (8, 1)).astype(np.uint16)


def unstriped(offs):
    return offs[:16].T.reshape(-1).astype(np.int64)


E2M1 = np.array([0.0, 0.5, 1.0, 1.5, 2.0, 3.0, 4.0, 6.0, -0.0, -0.5, -1.0, -1.5, -2.0, -3.0, -4.0, -6.0])


def pack_weight(w, fmt):
    k, n = w.shape
    w = f64(np.asarray(w, np.float32).astype(ml_dtypes.bfloat16)).reshape(k // 32, 32, n)
    amax = np.abs(w).max(1)
    if fmt == "e4m3":
        byte = np.frexp(amax)[1] - 1 + 127 - 7
    else:
        mant, ex = np.frexp(amax / 6.0)
        byte = np.where(mant > 0.5, ex, ex - 1) + 127
    byte = np.clip(np.where(amax > 0, byte, 1), 1, 254)
    scaled = (w * np.exp2(127.0 - byte)[:, None, :]).reshape(k, n).astype(np.float32)
    by_word = np.ascontiguousarray(scaled.reshape(k // 512, 128, 4, n).transpose(0, 1, 3, 2))
    if fmt == "e4m3":
        words = by_word.astype(ml_dtypes.float8_e4m3fn).view(np.uint8)
    else:
        c = by_word.astype(ml_dtypes.float4_e2m1fn).view(np.uint8) & 0xF
        words = (c[..., 0::2] | (c[..., 1::2] << 4)).reshape(k // 512, 128, 2 * n)
    return np.ascontiguousarray(words), np.ascontiguousarray(byte.astype(np.uint8).reshape(k // 512, 16, n))


def unpack_weight(words, scales, fmt):
    g, _, n = scales.shape
    words = np.ascontiguousarray(words).reshape(g, 128, n, -1)
    if fmt == "e4m3":
        vals = words.view(ml_dtypes.float8_e4m3fn).astype(np.float64)
    else:
        nib = np.empty((g, 128, n, 4), np.uint8)
        nib[..., 0::2] = words & 0xF
        nib[..., 1::2] = words >> 4
        vals = E2M1[nib]
    vals = vals * np.repeat(np.exp2(scales.astype(np.float64) - 127.0), 8, axis=1)[..., None]
    return vals.transpose(0, 1, 3, 2).reshape(g * 512, n)


K, R, T, M, J = 1024, 512, 2048, 512, 1024


def setup_inputs():
    n = np.random.standard_normal
    s = mx_kscale(K)[:, None]
    u = mx_kscale(R)[:, None]
    p_tab = pack_weight(n((K, T)) * s, "e4m3")
    p_wa = pack_weight(n((K, R)) / np.sqrt(K) / s, "e4m3")
    p_wb = pack_weight(n((K, R)) / np.sqrt(K) / s, "e4m3")
    return {
        "tab_words": p_tab[0],
        "tab_scales": p_tab[1],
        "wa_words": p_wa[0],
        "wa_scales": p_wa[1],
        "wb_words": p_wb[0],
        "wb_scales": p_wb[1],
        "sa": (np.random.uniform(0.5, 2.0, R) * u[:, 0]).astype(np.float32),
        "sb": (np.random.uniform(0.5, 2.0, R) / u[:, 0]).astype(np.float32),
        "offs": striped(np.random.permutation(T)[:M]),
        "offs2": striped(np.random.permutation(T)[:J]),
    }


def reference(tab_words, tab_scales, wa_words, wa_scales, wb_words, wb_scales, sa, sb, offs, offs2):
    idx = unstriped(offs)
    idx2 = unstriped(offs2)
    tab_ = unpack_weight(tab_words, tab_scales, "e4m3")[:, idx]
    tabb_ = unpack_weight(tab_words, tab_scales, "e4m3")[:, idx2]
    wa_ = unpack_weight(wa_words, wa_scales, "e4m3")
    wb_ = unpack_weight(wb_words, wb_scales, "e4m3")
    za = wa_.T @ tab_
    zb = wb_.T @ tabb_
    ha = f64(sa)[:, None] * np.tanh(za)
    hb = f64(sb)[:, None] * np.tanh(zb)
    ha_ = mxq(ha, 0, "e4m3")
    hb_ = mxq(hb, 0, "e4m3")
    y = ha_.T @ hb_
    return y * 0.03125

@@ -1,0 +1,184 @@
+from contextlib import ExitStack
+
+import concourse.mybir as mybir
+from concourse.masks import make_identity
+
+K, R, T, M, J = 1024, 512, 2048, 512, 1024
+FLOPS = 2 * K * R * (M + J) + 2 * R * M * J
+
+F32 = mybir.dt.float32
+BF16 = mybir.dt.bfloat16
+I32 = mybir.dt.int32
+U32 = mybir.dt.uint32
+U16 = mybir.dt.uint16
+U8 = mybir.dt.uint8
+FP8X4 = mybir.dt.float8_e4m3fn_x4
+ACT = mybir.ActivationFunctionType
+MULT = mybir.AluOpType.mult
+
+P = 128
+PASSES = 2
+PACK = 4
+BLOCK = 128
+CHUNK = 256
+OUT_SCALE = 0.03125
+
+
+def tile_list_biaff_tanh_none_kernel(
+    tc, tab_words, tab_scales, wa_words, wa_scales, wb_words, wb_scales, sa, sb, offs, offs2, out
+):
+    nc = tc.nc
+    with ExitStack() as ctx:
+        held = ctx.enter_context(tc.tile_pool(name="held", bufs=1))
+        ring = ctx.enter_context(tc.tile_pool(name="ring", bufs=3))
+        wide = ctx.enter_context(tc.tile_pool(name="wide", bufs=6))
+        const_psum = ctx.enter_context(tc.psum_pool(name="const_psum", bufs=1))
+        z_psum = ctx.enter_context(tc.psum_pool(name="z_psum", bufs=4))
+        y_psum = ctx.enter_context(tc.psum_pool(name="y_psum", bufs=3))
+
+        list_a = held.tile([P, M // 16], U16, name="list_a")
+        list_b = held.tile([P, J // 16], U16, name="list_b")
+        tab_plane = held.tile([P, T], U8, name="tab_plane", align_bytes=64)
+        w_plane_raw = [held.tile([P, R], U8, name="w_plane_raw%d" % s, align_bytes=64) for s in range(2)]
+        w_plane = [held.tile([P, R], U8, name="w_plane%d" % s, align_bytes=64) for s in range(2)]
+        tab = [held.tile([P, T], I32, name="tab%d" % a, align_bytes=64) for a in range(PASSES)]
+        w_codes = [held.tile([P, PASSES, R], U32, name="w_codes%d" % s, align_bytes=64) for s in range(2)]
+        ident = held.tile([P, P], F32, name="ident")
+        gain_rows = held.tile([P, P], F32, name="gain_rows")
+        gains = const_psum.tile([P, P], F32, name="gains")
+
+        def load_plane(queues, plane, scales):
+            for q in range(4):
+                queues[q % len(queues)].dma_start(
+                    out=plane[32 * q : 32 * q + 8, :].bitcast(I32),
+                    in_=scales[:, 4 * q : 4 * q + 4, :].bitcast(I32),
+                )
+
+        nc.gpsimd.memset(tab_plane[:].bitcast(I32), 0)
+        nc.sync.dma_start(list_a[:], offs)
+        load_plane((nc.scalar, nc.sync), tab_plane, tab_scales)
+        w_raw = [held.tile([P, PASSES, R], I32, name="w_raw%d" % s, align_bytes=64) for s in range(2)]
+        nc.sync.dma_start(out=w_raw[0][:], in_=wa_words.rearrange("a p r i -> p a (r i)").bitcast(I32))
+        nc.sync.dma_start(list_b[:], offs2)
+        nc.sync.dma_start(out=tab[0][:], in_=tab_words[0].rearrange("p t i -> p (t i)").bitcast(I32))
+        nc.gpsimd.memset(w_plane_raw[0][:].bitcast(I32), 0)
+        load_plane((nc.sync,), w_plane_raw[0], wa_scales)
+
+        zeros = held.tile([P, P], F32, name="zeros")
+        nc.gpsimd.memset(zeros[:], 0.0)
+        nc.scalar.activation(gain_rows[:], zeros[:], ACT.Tanh)
+        for s, vec in enumerate((sa, sb)):
+            nc.sync.dma_start(
+                out=gain_rows[PACK * s : PACK * s + PACK, :].rearrange("t (b i) -> t b i", i=8),
+                in_=vec.rearrange("(b t i) -> t b i", t=PACK, i=8),
+            )
+        nc.sync.dma_start(out=tab[1][:], in_=tab_words[1].rearrange("p t i -> p (t i)").bitcast(I32))
+        nc.gpsimd.memset(w_plane_raw[1][:].bitcast(I32), 0)
+        load_plane((nc.sync,), w_plane_raw[1], wb_scales)
+        nc.sync.dma_start(out=w_raw[1][:], in_=wb_words.rearrange("a p r i -> p a (r i)").bitcast(I32))
+        make_identity(nc, ident[:])
+        nc.tensor.transpose(gains[:], gain_rows[:], ident[:])
+
+        picked_plane = [
+            held.tile([P, n], U8, name="picked_plane%d" % s, align_bytes=64) for s, n in enumerate((M, J))
+        ]
+        for s, lst in enumerate((list_a, list_b)):
+            nc.vector.tensor_copy(picked_plane[s][:], tab_plane[:].indirect(lst[:]))
+
+        def permute_weights(s):
+            nc.vector.tensor_copy(
+                out=w_codes[s][:].bitcast(I32).rearrange("p a (t b i) -> p a t b i", t=PACK, i=8),
+                in_=w_raw[s][:].rearrange("p a (b t i) -> p a t b i", t=PACK, i=8),
+            )
+            nc.vector.tensor_copy(
+                out=w_plane[s][:].bitcast(I32).rearrange("p (t b i) -> p t b i", t=PACK, i=2),
+                in_=w_plane_raw[s][:].bitcast(I32).rearrange("p (b t i) -> p t b i", t=PACK, i=2),
+            )
+
+        permute_weights(0)
+
+        ha_codes = held.tile([P, M], U32, name="ha_codes", align_bytes=64)
+        ha_plane = held.tile([P, M], U8, name="ha_plane", align_bytes=64)
+
+        chunks = [(0, c) for c in range(M // CHUNK)] + [(1, c) for c in range(J // CHUNK)]
+        lists = (list_a, list_b)
+        tanh_tiles = {}
+
+        def hidden_sums(s, c):
+            banks = [z_psum.tile([P, PACK, BLOCK], F32, name="z") for h in range(CHUNK // BLOCK)]
+            for a in range(PASSES):
+                words = ring.tile([P, CHUNK], U32, name="picked%d" % a, align_bytes=64, bufs=2 + a)
+                nc.vector.tensor_copy(
+                    words[:], tab[a][:].bitcast(U32).indirect(lists[s][:, c * CHUNK // 16 : (c + 1) * CHUNK // 16])
+                )
+                for h, z in enumerate(banks):
+                    col = c * CHUNK + h * BLOCK
+                    for t in range(PACK):
+                        nc.tensor.matmul_mx(
+                            out=z[:, t, :],
+                            lhsT=w_codes[s][:, a, t * P : (t + 1) * P].bitcast(FP8X4),
+                            lhsT_scale=w_plane[s][4 * a :, t * P : (t + 1) * P],
+                            rhs=words[:, h * BLOCK : (h + 1) * BLOCK].bitcast(FP8X4),
+                            rhs_scale=picked_plane[s][4 * a :, col : col + BLOCK],
+                            start=(a == 0 and t == 0),
+                            stop=(a == PASSES - 1 and t == PACK - 1),
+                        )
+            th = ring.tile([P, CHUNK, PACK], F32, name="th")
+            for h, z in enumerate(banks):
+                nc.scalar.activation(th[:, h * BLOCK : (h + 1) * BLOCK, :], z[:].rearrange("p t n -> p n t"), ACT.Tanh)
+            tanh_tiles[(s, c)] = th
+
+        def quantise(s, col, width):
+            h16 = ring.tile([P, width, PACK], BF16, name="h16", align_bytes=64)
+            nc.vector.tensor_tensor(
+                out=h16[:],
+                in0=tanh_tiles[(s, col // CHUNK)][:, col % CHUNK : col % CHUNK + width, :],
+                in1=gains[:, PACK * s : PACK * s + PACK].unsqueeze(1).to_broadcast([P, width, PACK]),
+                op=MULT,
+            )
+            if s == 0:
+                codes = ha_codes[:, col : col + width]
+                plane = ha_plane[:, col : col + width]
+            else:
+                hb_codes = ring.tile([P, width], U32, name="hb_codes", align_bytes=64)
+                hb_plane = ring.tile([P, width], U8, name="hb_plane", align_bytes=64)
+                codes = hb_codes[:]
+                plane = hb_plane[:]
+            nc.vector.quantize_mx(out=codes.bitcast(FP8X4), scales=plane, in_=h16[:].rearrange("p n t -> p (n t)"))
+            return codes, plane
+
+        out_view = out.rearrange("(u p) j -> p u j", p=P)
+
+        def scores(col, width, codes, plane):
+            for half in range(2):
+                y = y_psum.tile([P, 2, width], F32, name="y")
+                for v in range(2):
+                    u = 2 * half + v
+                    nc.tensor.matmul_mx(
+                        out=y[:, v, :],
+                        lhsT=ha_codes[:, u * P : (u + 1) * P].bitcast(FP8X4),
+                        lhsT_scale=ha_plane[:, u * P : (u + 1) * P],
+                        rhs=codes.bitcast(FP8X4),
+                        rhs_scale=plane,
+                        start=True,
+                        stop=True,
+                    )
+                res = wide.tile([P, 2, width], F32, name="res")
+                if col + width == J and half == 1:
+                    nc.vector.tensor_scalar_mul(res[:], y[:], OUT_SCALE)
+                else:
+                    nc.scalar.activation(res[:], y[:], ACT.Copy, scale=OUT_SCALE)
+                nc.sync.dma_start(out=out_view[:, 2 * half : 2 * half + 2, col : col + width], in_=res[:])
+
+        for step in range(len(chunks) + 1):
+            if step < len(chunks):
+                if chunks[step] == (1, 0):
+                    permute_weights(1)
+                hidden_sums(*chunks[step])
+            if step >= 1:
+                s, c = chunks[step - 1]
+                width = BLOCK if step == len(chunks) else CHUNK
+                for col in range(c * CHUNK, (c + 1) * CHUNK, width):
+                    codes, plane = quantise(s, col, width)
+                    if s == 1:
+                        scores(col, width, codes, plane)

@@ -30,22 +30,22 @@ def tile_list_biaff_tanh_none_kernel(
     nc = tc.nc
     with ExitStack() as ctx:
         held = ctx.enter_context(tc.tile_pool(name="held", bufs=1))
+        big = ctx.enter_context(tc.tile_pool(name="big", bufs=1))
         ring = ctx.enter_context(tc.tile_pool(name="ring", bufs=3))
         wide = ctx.enter_context(tc.tile_pool(name="wide", bufs=6))
         const_psum = ctx.enter_context(tc.psum_pool(name="const_psum", bufs=1))
-        z_psum = ctx.enter_context(tc.psum_pool(name="z_psum", bufs=4))
-        y_psum = ctx.enter_context(tc.psum_pool(name="y_psum", bufs=3))
+        z_psum = ctx.enter_context(tc.psum_pool(name="z_psum", bufs=3))
+        y_psum = ctx.enter_context(tc.psum_pool(name="y_psum", bufs=4))
 
         list_a = held.tile([P, M // 16], U16, name="list_a")
         list_b = held.tile([P, J // 16], U16, name="list_b")
         tab_plane = held.tile([P, T], U8, name="tab_plane", align_bytes=64)
-        w_plane_raw = [held.tile([P, R], U8, name="w_plane_raw%d" % s, align_bytes=64) for s in range(2)]
         w_plane = [held.tile([P, R], U8, name="w_plane%d" % s, align_bytes=64) for s in range(2)]
-        tab = [held.tile([P, T], I32, name="tab%d" % a, align_bytes=64) for a in range(PASSES)]
-        w_codes = [held.tile([P, PASSES, R], U32, name="w_codes%d" % s, align_bytes=64) for s in range(2)]
+        w_codes = [
+            [held.tile([P, R], U32, name="w_codes%d%d" % (s, a), align_bytes=64) for a in range(PASSES)]
+            for s in range(2)
+        ]
         ident = held.tile([P, P], F32, name="ident")
-        gain_rows = held.tile([P, P], F32, name="gain_rows")
-        gains = const_psum.tile([P, P], F32, name="gains")
 
         def load_plane(queues, plane, scales):
             for q in range(4):
@@ -54,30 +54,39 @@ def tile_list_biaff_tanh_none_kernel(
                     in_=scales[:, 4 * q : 4 * q + 4, :].bitcast(I32),
                 )
 
-        nc.gpsimd.memset(tab_plane[:].bitcast(I32), 0)
+        nc.vector.memset(tab_plane[:].bitcast(I32), 0)
         nc.sync.dma_start(list_a[:], offs)
-        load_plane((nc.scalar, nc.sync), tab_plane, tab_scales)
-        w_raw = [held.tile([P, PASSES, R], I32, name="w_raw%d" % s, align_bytes=64) for s in range(2)]
-        nc.sync.dma_start(out=w_raw[0][:], in_=wa_words.rearrange("a p r i -> p a (r i)").bitcast(I32))
+        load_plane((nc.sync,), tab_plane, tab_scales)
         nc.sync.dma_start(list_b[:], offs2)
-        nc.sync.dma_start(out=tab[0][:], in_=tab_words[0].rearrange("p t i -> p (t i)").bitcast(I32))
-        nc.gpsimd.memset(w_plane_raw[0][:].bitcast(I32), 0)
-        load_plane((nc.sync,), w_plane_raw[0], wa_scales)
 
-        zeros = held.tile([P, P], F32, name="zeros")
-        nc.gpsimd.memset(zeros[:], 0.0)
+        w_bytes = 4 * PASSES * R
+        blank = big.tile([P, R // 4], I32, name="blank", offset=w_bytes - R // 2)
+        nc.vector.memset(blank[:], 0)
+        w_plane_raw = held.tile([P, R], U8, name="w_plane_raw", align_bytes=64)
+        nc.vector.tensor_copy(w_plane_raw[:].bitcast(I32), blank[:])
+        zeros = big.tile([P, P], F32, name="zeros", offset=w_bytes + PASSES * 4 * T - 2 * P)
+        gain_rows = held.tile([P, P], F32, name="gain_rows")
+        nc.vector.memset(zeros[:], 0.0)
         nc.scalar.activation(gain_rows[:], zeros[:], ACT.Tanh)
+        tab = [
+            big.tile([P, T], I32, name="tab%d" % a, offset=w_bytes + a * 4 * T, align_bytes=64) for a in range(PASSES)
+        ]
+        w_raw = [
+            big.tile([P, PASSES, R], I32, name="w_raw%d" % s, offset=s * (w_bytes + PASSES * 4 * T), align_bytes=64)
+            for s in range(2)
+        ]
+        nc.sync.dma_start(out=tab[0][:], in_=tab_words[0].rearrange("p t i -> p (t i)").bitcast(I32))
+        nc.sync.dma_start(out=w_raw[0][:], in_=wa_words.rearrange("a p r i -> p a (r i)").bitcast(I32))
+        load_plane((nc.sync,), w_plane_raw, wa_scales)
+        nc.sync.dma_start(out=tab[1][:], in_=tab_words[1].rearrange("p t i -> p (t i)").bitcast(I32))
+        nc.sync.dma_start(out=w_raw[1][:], in_=wb_words.rearrange("a p r i -> p a (r i)").bitcast(I32))
+
+        make_identity(nc, ident[:])
         for s, vec in enumerate((sa, sb)):
-            nc.sync.dma_start(
+            nc.gpsimd.dma_start(
                 out=gain_rows[PACK * s : PACK * s + PACK, :].rearrange("t (b i) -> t b i", i=8),
                 in_=vec.rearrange("(b t i) -> t b i", t=PACK, i=8),
             )
-        nc.sync.dma_start(out=tab[1][:], in_=tab_words[1].rearrange("p t i -> p (t i)").bitcast(I32))
-        nc.gpsimd.memset(w_plane_raw[1][:].bitcast(I32), 0)
-        load_plane((nc.sync,), w_plane_raw[1], wb_scales)
-        nc.sync.dma_start(out=w_raw[1][:], in_=wb_words.rearrange("a p r i -> p a (r i)").bitcast(I32))
-        make_identity(nc, ident[:])
-        nc.tensor.transpose(gains[:], gain_rows[:], ident[:])
 
         picked_plane = [
             held.tile([P, n], U8, name="picked_plane%d" % s, align_bytes=64) for s, n in enumerate((M, J))
@@ -86,16 +95,19 @@ def tile_list_biaff_tanh_none_kernel(
             nc.vector.tensor_copy(picked_plane[s][:], tab_plane[:].indirect(lst[:]))
 
         def permute_weights(s):
-            nc.vector.tensor_copy(
-                out=w_codes[s][:].bitcast(I32).rearrange("p a (t b i) -> p a t b i", t=PACK, i=8),
-                in_=w_raw[s][:].rearrange("p a (b t i) -> p a t b i", t=PACK, i=8),
-            )
-            nc.vector.tensor_copy(
-                out=w_plane[s][:].bitcast(I32).rearrange("p (t b i) -> p t b i", t=PACK, i=2),
-                in_=w_plane_raw[s][:].bitcast(I32).rearrange("p (b t i) -> p t b i", t=PACK, i=2),
-            )
+            for a in range(PASSES):
+                nc.gpsimd.tensor_copy(
+                    out=w_codes[s][a][:].bitcast(I32).rearrange("p (t b i) -> p t b i", t=PACK, i=8),
+                    in_=w_raw[s][:, a, :].rearrange("p (b t i) -> p t b i", t=PACK, i=8),
+                )
+                if a == 0:
+                    nc.gpsimd.tensor_copy(
+                        out=w_plane[s][:].bitcast(I32).rearrange("p (t b i) -> p t b i", t=PACK, i=2),
+                        in_=w_plane_raw[:].bitcast(I32).rearrange("p (b t i) -> p t b i", t=PACK, i=2),
+                    )
 
         permute_weights(0)
+        load_plane((nc.sync,), w_plane_raw, wb_scales)
 
         ha_codes = held.tile([P, M], U32, name="ha_codes", align_bytes=64)
         ha_plane = held.tile([P, M], U8, name="ha_plane", align_bytes=64)
@@ -105,9 +117,11 @@ def tile_list_biaff_tanh_none_kernel(
         tanh_tiles = {}
 
         def hidden_sums(s, c):
-            banks = [z_psum.tile([P, PACK, BLOCK], F32, name="z") for h in range(CHUNK // BLOCK)]
+            banks = [z_psum.tile([P, PACK, BLOCK], F32, name="z") for h in range(CHUNK // BLOCK - ((s, c) == (0, 0)))]
+            if (s, c) == (0, 0):
+                banks.insert(0, const_psum.tile([P, PACK, BLOCK], F32, name="first_z", tag="fixed"))
             for a in range(PASSES):
-                words = ring.tile([P, CHUNK], U32, name="picked%d" % a, align_bytes=64, bufs=2 + a)
+                words = ring.tile([P, CHUNK], U32, name="picked%d" % a, align_bytes=64, bufs=4 - a)
                 nc.vector.tensor_copy(
                     words[:], tab[a][:].bitcast(U32).indirect(lists[s][:, c * CHUNK // 16 : (c + 1) * CHUNK // 16])
                 )
@@ -116,19 +130,19 @@ def tile_list_biaff_tanh_none_kernel(
                     for t in range(PACK):
                         nc.tensor.matmul_mx(
                             out=z[:, t, :],
-                            lhsT=w_codes[s][:, a, t * P : (t + 1) * P].bitcast(FP8X4),
+                            lhsT=w_codes[s][a][:, t * P : (t + 1) * P].bitcast(FP8X4),
                             lhsT_scale=w_plane[s][4 * a :, t * P : (t + 1) * P],
                             rhs=words[:, h * BLOCK : (h + 1) * BLOCK].bitcast(FP8X4),
                             rhs_scale=picked_plane[s][4 * a :, col : col + BLOCK],
                             start=(a == 0 and t == 0),
                             stop=(a == PASSES - 1 and t == PACK - 1),
                         )
-            th = ring.tile([P, CHUNK, PACK], F32, name="th")
+            th = wide.tile([P, CHUNK, PACK], F32, name="th")
             for h, z in enumerate(banks):
                 nc.scalar.activation(th[:, h * BLOCK : (h + 1) * BLOCK, :], z[:].rearrange("p t n -> p n t"), ACT.Tanh)
             tanh_tiles[(s, c)] = th
 
-        def quantise(s, col, width):
+        def quantise(gains, s, col, width):
             h16 = ring.tile([P, width, PACK], BF16, name="h16", align_bytes=64)
             nc.vector.tensor_tensor(
                 out=h16[:],
@@ -170,15 +184,19 @@ def tile_list_biaff_tanh_none_kernel(
                     nc.scalar.activation(res[:], y[:], ACT.Copy, scale=OUT_SCALE)
                 nc.sync.dma_start(out=out_view[:, 2 * half : 2 * half + 2, col : col + width], in_=res[:])
 
+        gains = None
         for step in range(len(chunks) + 1):
             if step < len(chunks):
                 if chunks[step] == (1, 0):
                     permute_weights(1)
                 hidden_sums(*chunks[step])
+                if step == 0:
+                    gains = const_psum.tile([P, P], F32, name="gains", tag="fixed")
+                    nc.tensor.transpose(gains[:], gain_rows[:], ident[:])
             if step >= 1:
                 s, c = chunks[step - 1]
                 width = BLOCK if step == len(chunks) else CHUNK
                 for col in range(c * CHUNK, (c + 1) * CHUNK, width):
-                    codes, plane = quantise(s, col, width)
+                    codes, plane = quantise(gains, s, col, width)
                     if s == 1:
                         scores(col, width, codes, plane)

@@ -1,7 +1,6 @@
 from contextlib import ExitStack
 
 import concourse.mybir as mybir
-from concourse.masks import make_identity
 
 K, R, T, M, J = 1024, 512, 2048, 512, 1024
 FLOPS = 2 * K * R * (M + J) + 2 * R * M * J
@@ -22,6 +21,7 @@ PACK = 4
 BLOCK = 128
 CHUNK = 256
 OUT_SCALE = 0.03125
+GPSIMD_COLUMNS = 384
 
 
 def tile_list_biaff_tanh_none_kernel(
@@ -59,29 +59,38 @@ def tile_list_biaff_tanh_none_kernel(
         load_plane((nc.sync,), tab_plane, tab_scales)
         nc.sync.dma_start(list_b[:], offs2)
 
-        w_bytes = 4 * PASSES * R
-        blank = big.tile([P, R // 4], I32, name="blank", offset=w_bytes - R // 2)
+        wa_raw = held.tile([P, PASSES, R], I32, name="wa_raw", align_bytes=64)
+        nc.scalar.dma_start(out=wa_raw[:], in_=wa_words.rearrange("a p r i -> p a (r i)").bitcast(I32))
+        tab_end = PASSES * 4 * T
+        blank = big.tile([P, R // 4], I32, name="blank", offset=0)
         nc.vector.memset(blank[:], 0)
-        w_plane_raw = held.tile([P, R], U8, name="w_plane_raw", align_bytes=64)
-        nc.vector.tensor_copy(w_plane_raw[:].bitcast(I32), blank[:])
-        zeros = big.tile([P, P], F32, name="zeros", offset=w_bytes + PASSES * 4 * T - 2 * P)
+        wa_plane_raw = held.tile([P, R], U8, name="wa_plane_raw", align_bytes=64)
+        nc.vector.tensor_copy(wa_plane_raw[:].bitcast(I32), blank[:])
+        zeros = big.tile([P, 2 * P], F32, name="zeros", offset=tab_end - 2 * P)
         gain_rows = held.tile([P, P], F32, name="gain_rows")
         nc.vector.memset(zeros[:], 0.0)
-        nc.scalar.activation(gain_rows[:], zeros[:], ACT.Tanh)
-        tab = [
-            big.tile([P, T], I32, name="tab%d" % a, offset=w_bytes + a * 4 * T, align_bytes=64) for a in range(PASSES)
-        ]
-        w_raw = [
-            big.tile([P, PASSES, R], I32, name="w_raw%d" % s, offset=s * (w_bytes + PASSES * 4 * T), align_bytes=64)
-            for s in range(2)
-        ]
+        nc.scalar.activation(gain_rows[:], zeros[:, 0:P], ACT.Tanh)
+        nc.gpsimd.affine_select(
+            out=ident[:],
+            in_=zeros[:, P : 2 * P],
+            compare_op=mybir.AluOpType.not_equal,
+            fill=1.0,
+            base=0,
+            pattern=[[-1, P]],
+            channel_multiplier=1,
+        )
+        tab = [big.tile([P, T], I32, name="tab%d" % a, offset=a * 4 * T, align_bytes=64) for a in range(PASSES)]
+        wb_plane_raw = big.tile([P, R], U8, name="wb_plane_raw", offset=tab_end, align_bytes=64)
+        wb_raw = big.tile([P, PASSES, R], I32, name="wb_raw", offset=tab_end + R, align_bytes=64)
+        w_raw = (wa_raw, wb_raw)
+        w_plane_raw = (wa_plane_raw, wb_plane_raw)
         nc.sync.dma_start(out=tab[0][:], in_=tab_words[0].rearrange("p t i -> p (t i)").bitcast(I32))
-        nc.sync.dma_start(out=w_raw[0][:], in_=wa_words.rearrange("a p r i -> p a (r i)").bitcast(I32))
-        load_plane((nc.sync,), w_plane_raw, wa_scales)
+        load_plane((nc.sync,), wa_plane_raw, wa_scales)
         nc.sync.dma_start(out=tab[1][:], in_=tab_words[1].rearrange("p t i -> p (t i)").bitcast(I32))
-        nc.sync.dma_start(out=w_raw[1][:], in_=wb_words.rearrange("a p r i -> p a (r i)").bitcast(I32))
+        nc.sync.dma_start(out=wb_raw[:], in_=wb_words.rearrange("a p r i -> p a (r i)").bitcast(I32))
+        nc.vector.memset(wb_plane_raw[:].bitcast(I32), 0)
+        load_plane((nc.sync,), wb_plane_raw, wb_scales)
 
-        make_identity(nc, ident[:])
         for s, vec in enumerate((sa, sb)):
             nc.gpsimd.dma_start(
                 out=gain_rows[PACK * s : PACK * s + PACK, :].rearrange("t (b i) -> t b i", i=8),
@@ -103,16 +112,15 @@ def tile_list_biaff_tanh_none_kernel(
                 if a == 0:
                     nc.gpsimd.tensor_copy(
                         out=w_plane[s][:].bitcast(I32).rearrange("p (t b i) -> p t b i", t=PACK, i=2),
-                        in_=w_plane_raw[:].bitcast(I32).rearrange("p (b t i) -> p t b i", t=PACK, i=2),
+                        in_=w_plane_raw[s][:].bitcast(I32).rearrange("p (b t i) -> p t b i", t=PACK, i=2),
                     )
 
         permute_weights(0)
-        load_plane((nc.sync,), w_plane_raw, wb_scales)
+        permute_weights(1)
 
-        ha_codes = held.tile([P, M], U32, name="ha_codes", align_bytes=64)
+        ha_codes = big.tile([P, M], U32, name="ha_codes", offset=4 * T, align_bytes=64)
         ha_plane = held.tile([P, M], U8, name="ha_plane", align_bytes=64)
 
-        chunks = [(0, c) for c in range(M // CHUNK)] + [(1, c) for c in range(J // CHUNK)]
         lists = (list_a, list_b)
         tanh_tiles = {}
 
@@ -121,7 +129,7 @@ def tile_list_biaff_tanh_none_kernel(
             if (s, c) == (0, 0):
                 banks.insert(0, const_psum.tile([P, PACK, BLOCK], F32, name="first_z", tag="fixed"))
             for a in range(PASSES):
-                words = ring.tile([P, CHUNK], U32, name="picked%d" % a, align_bytes=64, bufs=4 - a)
+                words = ring.tile([P, CHUNK], U32, name="picked", align_bytes=64, bufs=5)
                 nc.vector.tensor_copy(
                     words[:], tab[a][:].bitcast(U32).indirect(lists[s][:, c * CHUNK // 16 : (c + 1) * CHUNK // 16])
                 )
@@ -142,23 +150,33 @@ def tile_list_biaff_tanh_none_kernel(
                 nc.scalar.activation(th[:, h * BLOCK : (h + 1) * BLOCK, :], z[:].rearrange("p t n -> p n t"), ACT.Tanh)
             tanh_tiles[(s, c)] = th
 
-        def quantise(gains, s, col, width):
-            h16 = ring.tile([P, width, PACK], BF16, name="h16", align_bytes=64)
-            nc.vector.tensor_tensor(
-                out=h16[:],
+        def apply_gain(engine, gain, s, col, width, h16):
+            engine.tensor_tensor(
+                out=h16,
                 in0=tanh_tiles[(s, col // CHUNK)][:, col % CHUNK : col % CHUNK + width, :],
-                in1=gains[:, PACK * s : PACK * s + PACK].unsqueeze(1).to_broadcast([P, width, PACK]),
+                in1=gain[:, PACK * s : PACK * s + PACK].unsqueeze(1).to_broadcast([P, width, PACK]),
                 op=MULT,
             )
-            if s == 0:
-                codes = ha_codes[:, col : col + width]
-                plane = ha_plane[:, col : col + width]
-            else:
-                hb_codes = ring.tile([P, width], U32, name="hb_codes", align_bytes=64)
-                hb_plane = ring.tile([P, width], U8, name="hb_plane", align_bytes=64)
-                codes = hb_codes[:]
-                plane = hb_plane[:]
-            nc.vector.quantize_mx(out=codes.bitcast(FP8X4), scales=plane, in_=h16[:].rearrange("p n t -> p (n t)"))
+
+        def quantise_a(gains, gains_sb):
+            h16 = big.tile([P, M, PACK], BF16, name="ha16", offset=tab_end, align_bytes=64)
+            for col in range(0, M, BLOCK):
+                if col < GPSIMD_COLUMNS:
+                    apply_gain(nc.gpsimd, gains_sb, 0, col, BLOCK, h16[:, col : col + BLOCK, :])
+                else:
+                    apply_gain(nc.vector, gains, 0, col, BLOCK, h16[:, col : col + BLOCK, :])
+            nc.vector.quantize_mx(
+                out=ha_codes[:].bitcast(FP8X4), scales=ha_plane[:], in_=h16[:].rearrange("p n t -> p (n t)")
+            )
+
+        def quantise_b(gains, col, width):
+            h16 = ring.tile([P, width, PACK], BF16, name="hb16", align_bytes=64)
+            apply_gain(nc.vector, gains, 1, col, width, h16[:])
+            codes = ring.tile([P, width], U32, name="hb_codes", align_bytes=64)
+            plane = ring.tile([P, width], U8, name="hb_plane", align_bytes=64)
+            nc.vector.quantize_mx(
+                out=codes[:].bitcast(FP8X4), scales=plane[:], in_=h16[:].rearrange("p n t -> p (n t)")
+            )
             return codes, plane
 
         out_view = out.rearrange("(u p) j -> p u j", p=P)
@@ -172,8 +190,8 @@ def tile_list_biaff_tanh_none_kernel(
                         out=y[:, v, :],
                         lhsT=ha_codes[:, u * P : (u + 1) * P].bitcast(FP8X4),
                         lhsT_scale=ha_plane[:, u * P : (u + 1) * P],
-                        rhs=codes.bitcast(FP8X4),
-                        rhs_scale=plane,
+                        rhs=codes[:].bitcast(FP8X4),
+                        rhs_scale=plane[:],
                         start=True,
                         stop=True,
                     )
@@ -184,19 +202,18 @@ def tile_list_biaff_tanh_none_kernel(
                     nc.scalar.activation(res[:], y[:], ACT.Copy, scale=OUT_SCALE)
                 nc.sync.dma_start(out=out_view[:, 2 * half : 2 * half + 2, col : col + width], in_=res[:])
 
-        gains = None
-        for step in range(len(chunks) + 1):
-            if step < len(chunks):
-                if chunks[step] == (1, 0):
-                    permute_weights(1)
-                hidden_sums(*chunks[step])
-                if step == 0:
-                    gains = const_psum.tile([P, P], F32, name="gains", tag="fixed")
-                    nc.tensor.transpose(gains[:], gain_rows[:], ident[:])
-            if step >= 1:
-                s, c = chunks[step - 1]
-                width = BLOCK if step == len(chunks) else CHUNK
-                for col in range(c * CHUNK, (c + 1) * CHUNK, width):
-                    codes, plane = quantise(gains, s, col, width)
-                    if s == 1:
-                        scores(col, width, codes, plane)
+        hidden_sums(0, 0)
+        gains = const_psum.tile([P, P], F32, name="gains", tag="fixed")
+        nc.tensor.transpose(gains[:], gain_rows[:], ident[:])
+        gains_sb = held.tile([P, PACK], F32, name="gains_sb")
+        nc.scalar.copy(gains_sb[:], gains[:, 0:PACK])
+        hidden_sums(0, 1)
+        for c in range(J // CHUNK):
+            hidden_sums(1, c)
+        quantise_a(gains, gains_sb)
+        last = J // CHUNK - 1
+        for c in range(J // CHUNK):
+            width = BLOCK if c == last else CHUNK
+            for col in range(c * CHUNK, (c + 1) * CHUNK, width):
+                codes, plane = quantise_b(gains, col, width)
+                scores(col, width, codes, plane)

@@ -21,7 +21,9 @@ PACK = 4
 BLOCK = 128
 CHUNK = 256
 OUT_SCALE = 0.03125
-GPSIMD_COLUMNS = 384
+W_WORDS = PASSES * R
+W_RAW = W_WORDS + R // 4
+AHEAD = 4
 
 
 def tile_list_biaff_tanh_none_kernel(
@@ -31,189 +33,234 @@ def tile_list_biaff_tanh_none_kernel(
     with ExitStack() as ctx:
         held = ctx.enter_context(tc.tile_pool(name="held", bufs=1))
         big = ctx.enter_context(tc.tile_pool(name="big", bufs=1))
-        ring = ctx.enter_context(tc.tile_pool(name="ring", bufs=3))
-        wide = ctx.enter_context(tc.tile_pool(name="wide", bufs=6))
+        picks = ctx.enter_context(tc.tile_pool(name="picks", bufs=1))
+        ring = ctx.enter_context(tc.tile_pool(name="ring", bufs=4))
+        tanhs = ctx.enter_context(tc.tile_pool(name="tanhs", bufs=1))
+        wide = ctx.enter_context(tc.tile_pool(name="wide", bufs=10))
         const_psum = ctx.enter_context(tc.psum_pool(name="const_psum", bufs=1))
-        z_psum = ctx.enter_context(tc.psum_pool(name="z_psum", bufs=3))
-        y_psum = ctx.enter_context(tc.psum_pool(name="y_psum", bufs=4))
+        banks = ctx.enter_context(tc.psum_pool(name="banks", bufs=7))
 
         list_a = held.tile([P, M // 16], U16, name="list_a")
         list_b = held.tile([P, J // 16], U16, name="list_b")
+        lists = (list_a, list_b)
         tab_plane = held.tile([P, T], U8, name="tab_plane", align_bytes=64)
         w_plane = [held.tile([P, R], U8, name="w_plane%d" % s, align_bytes=64) for s in range(2)]
         w_codes = [
             [held.tile([P, R], U32, name="w_codes%d%d" % (s, a), align_bytes=64) for a in range(PASSES)]
             for s in range(2)
         ]
-        ident = held.tile([P, P], F32, name="ident")
+        gain_rows = held.tile([P, P], F32, name="gain_rows")
 
-        def load_plane(queues, plane, scales):
+        def load_plane(plane, scales):
             for q in range(4):
-                queues[q % len(queues)].dma_start(
-                    out=plane[32 * q : 32 * q + 8, :].bitcast(I32),
-                    in_=scales[:, 4 * q : 4 * q + 4, :].bitcast(I32),
-                )
+                nc.sync.dma_start(out=plane[32 * q : 32 * q + 8, :], in_=scales[:, 4 * q : 4 * q + 4, :].bitcast(I32))
 
+        def load_words(raw, words):
+            nc.sync.dma_start(
+                out=raw.rearrange("p (a r) -> p a r", a=PASSES), in_=words.rearrange("a p r i -> p a (r i)").bitcast(I32)
+            )
+
+        tab_at = R
+        wb_at = tab_at + PASSES * 4 * T
         nc.vector.memset(tab_plane[:].bitcast(I32), 0)
         nc.sync.dma_start(list_a[:], offs)
-        load_plane((nc.sync,), tab_plane, tab_scales)
+        wa_raw = held.tile([P, W_WORDS], I32, name="wa_raw", align_bytes=64)
+        load_words(wa_raw[:], wa_words)
+        load_plane(tab_plane[:].bitcast(I32), tab_scales)
         nc.sync.dma_start(list_b[:], offs2)
 
-        wa_raw = held.tile([P, PASSES, R], I32, name="wa_raw", align_bytes=64)
-        nc.scalar.dma_start(out=wa_raw[:], in_=wa_words.rearrange("a p r i -> p a (r i)").bitcast(I32))
-        tab_end = PASSES * 4 * T
-        blank = big.tile([P, R // 4], I32, name="blank", offset=0)
-        nc.vector.memset(blank[:], 0)
-        wa_plane_raw = held.tile([P, R], U8, name="wa_plane_raw", align_bytes=64)
-        nc.vector.tensor_copy(wa_plane_raw[:].bitcast(I32), blank[:])
-        zeros = big.tile([P, 2 * P], F32, name="zeros", offset=tab_end - 2 * P)
-        gain_rows = held.tile([P, P], F32, name="gain_rows")
-        nc.vector.memset(zeros[:], 0.0)
-        nc.scalar.activation(gain_rows[:], zeros[:, 0:P], ACT.Tanh)
+        gain_row = (0, PACK)
+
+        def load_gain(s, vec):
+            nc.sync.dma_start(
+                out=gain_rows[gain_row[s] : gain_row[s] + PACK, :].rearrange("t (b i) -> t b i", i=8),
+                in_=vec.rearrange("(b t i) -> t b i", t=PACK, i=8),
+            )
+
+        zeros_early = big.tile([P, P], F32, name="zeros_early", offset=tab_at - 2 * P)
+        nc.gpsimd.memset(zeros_early[:], 0.0)
+        nc.gpsimd.tensor_copy(gain_rows[:], zeros_early[:])
+        zeros_late = big.tile([P, P], F32, name="zeros_late", offset=wb_at - 2 * P)
+        nc.vector.memset(zeros_late[:], 0.0)
+        blank = held.tile([P, P], F32, name="blank")
+        nc.scalar.activation(blank[:], zeros_late[:], ACT.Tanh)
+
+        wa_plane_raw = big.tile([P, R // 4], I32, name="wa_plane_raw", offset=0, align_bytes=64)
+        wb_raw = big.tile([P, W_RAW], I32, name="wb_raw", offset=wb_at, align_bytes=64)
+        raw_words = ((wa_raw[:, 0:R], wa_raw[:, R:W_WORDS]), (wb_raw[:, 0:R], wb_raw[:, R:W_WORDS]))
+        raw_plane = (wa_plane_raw[:], wb_raw[:, W_WORDS:W_RAW])
+        tab = [big.tile([P, T], I32, name="tab%d" % a, offset=tab_at + a * 4 * T, align_bytes=64) for a in range(PASSES)]
+
+        def load_table(a):
+            nc.sync.dma_start(out=tab[a][:], in_=tab_words[a].rearrange("p t i -> p (t i)").bitcast(I32))
+
+        load_table(0)
+        nc.gpsimd.memset(raw_plane[0], 0)
+        load_plane(raw_plane[0], wa_scales)
+        load_gain(0, sa)
+        load_gain(1, sb)
+        load_table(1)
+        nc.gpsimd.memset(raw_plane[1], 0)
+        load_plane(raw_plane[1], wb_scales)
+        for a in range(PASSES):
+            nc.sync.dma_start(out=raw_words[1][a], in_=wb_words[a].rearrange("p r i -> p (r i)").bitcast(I32))
+
+        HALF = J // 2
+        picked_plane = {}
+
+        def gather_plane(s, start, tile):
+            nc.vector.tensor_copy(tile[:], tab_plane[:].indirect(lists[s][:, start // 16 : (start + HALF) // 16]))
+            picked_plane[(s, start // HALF)] = tile
+
+        for s in range(2):
+            gather_plane(s, 0, held.tile([P, HALF], U8, name="picked_plane%d" % s, align_bytes=64))
+
+        for s in range(2):
+            for a in range(PASSES):
+                nc.gpsimd.tensor_copy(
+                    out=w_codes[s][a][:].bitcast(I32).rearrange("p (t b i) -> p t b i", t=PACK, i=8),
+                    in_=raw_words[s][a].rearrange("p (b t i) -> p t b i", t=PACK, i=8),
+                )
+                if a == 0:
+                    nc.gpsimd.tensor_copy(
+                        out=w_plane[s][:].bitcast(I32).rearrange("p (t b i) -> p t b i", t=PACK, i=2),
+                        in_=raw_plane[s].rearrange("p (b t i) -> p t b i", t=PACK, i=2),
+                    )
+
+        chunks = [(0, c) for c in range(M // CHUNK)] + [(1, c) for c in range(J // CHUNK)]
+        picked = {}
+
+        def gather_words(i, a, slot):
+            s, c = chunks[i]
+            words = picks.tile([P, CHUNK], U32, name="picked%d%d" % (i, a), offset=4 * CHUNK * slot, align_bytes=64)
+            nc.vector.tensor_copy(
+                words[:], tab[a][:].bitcast(U32).indirect(lists[s][:, c * CHUNK // 16 : (c + 1) * CHUNK // 16])
+            )
+            picked[(i, a)] = words
+
+        for a in range(PASSES):
+            for i in range(AHEAD):
+                gather_words(i, a, a * AHEAD + i)
+        gather_plane(1, HALF, picks.tile([P, HALF], U8, name="picked_plane2", offset=4 * CHUNK * AHEAD, align_bytes=64))
+        freed = [a * AHEAD + i for i in range(1, AHEAD) for a in range(PASSES)][1:]
+        for n, (i, a) in enumerate([(i, a) for i in range(AHEAD, len(chunks)) for a in range(PASSES)]):
+            gather_words(i, a, freed[n])
+
+        tanh_tiles = {}
+        sums = {}
+
+        def first_stage(i, a):
+            s, c = chunks[i]
+            for h in range(CHUNK // BLOCK):
+                if a == 0:
+                    sums[(i, h)] = banks.tile([P, PACK, BLOCK], F32, name="bank")
+                col = c * CHUNK + h * BLOCK
+                for t in range(PACK):
+                    nc.tensor.matmul_mx(
+                        out=sums[(i, h)][:, t, :],
+                        lhsT=w_codes[s][a][:, t * P : (t + 1) * P].bitcast(FP8X4),
+                        lhsT_scale=w_plane[s][4 * a :, t * P : (t + 1) * P],
+                        rhs=picked[(i, a)][:, h * BLOCK : (h + 1) * BLOCK].bitcast(FP8X4),
+                        rhs_scale=picked_plane[(s, col // HALF)][4 * a :, col % HALF : col % HALF + BLOCK],
+                        start=(a == 0 and t == 0),
+                        stop=(a == PASSES - 1 and t == PACK - 1),
+                    )
+            if a == PASSES - 1:
+                th = tanhs.tile([P, CHUNK, PACK], F32, name="th%d" % i, offset=i * 4 * PACK * CHUNK, align_bytes=64)
+                for h in range(CHUNK // BLOCK):
+                    nc.scalar.activation(
+                        th[:, h * BLOCK : (h + 1) * BLOCK, :], sums[(i, h)][:].rearrange("p t n -> p n t"), ACT.Tanh
+                    )
+                tanh_tiles[i] = th
+
+        ident = held.tile([P, P], F32, name="ident")
         nc.gpsimd.affine_select(
             out=ident[:],
-            in_=zeros[:, P : 2 * P],
+            in_=blank[:],
             compare_op=mybir.AluOpType.not_equal,
             fill=1.0,
             base=0,
             pattern=[[-1, P]],
             channel_multiplier=1,
         )
-        tab = [big.tile([P, T], I32, name="tab%d" % a, offset=a * 4 * T, align_bytes=64) for a in range(PASSES)]
-        wb_plane_raw = big.tile([P, R], U8, name="wb_plane_raw", offset=tab_end, align_bytes=64)
-        wb_raw = big.tile([P, PASSES, R], I32, name="wb_raw", offset=tab_end + R, align_bytes=64)
-        w_raw = (wa_raw, wb_raw)
-        w_plane_raw = (wa_plane_raw, wb_plane_raw)
-        nc.sync.dma_start(out=tab[0][:], in_=tab_words[0].rearrange("p t i -> p (t i)").bitcast(I32))
-        load_plane((nc.sync,), wa_plane_raw, wa_scales)
-        nc.sync.dma_start(out=tab[1][:], in_=tab_words[1].rearrange("p t i -> p (t i)").bitcast(I32))
-        nc.sync.dma_start(out=wb_raw[:], in_=wb_words.rearrange("a p r i -> p a (r i)").bitcast(I32))
-        nc.vector.memset(wb_plane_raw[:].bitcast(I32), 0)
-        load_plane((nc.sync,), wb_plane_raw, wb_scales)
+        gains = const_psum.tile([P, P], F32, name="gains")
+        nc.tensor.transpose(gains[:], gain_rows[:], ident[:])
+        gains_a = held.tile([P, BLOCK, PACK], F32, name="gains_a")
+        nc.scalar.copy(gains_a[:], gains[:, gain_row[0] : gain_row[0] + PACK].unsqueeze(1).to_broadcast([P, BLOCK, PACK]))
 
-        for s, vec in enumerate((sa, sb)):
-            nc.gpsimd.dma_start(
-                out=gain_rows[PACK * s : PACK * s + PACK, :].rearrange("t (b i) -> t b i", i=8),
-                in_=vec.rearrange("(b t i) -> t b i", t=PACK, i=8),
-            )
-
-        picked_plane = [
-            held.tile([P, n], U8, name="picked_plane%d" % s, align_bytes=64) for s, n in enumerate((M, J))
-        ]
-        for s, lst in enumerate((list_a, list_b)):
-            nc.vector.tensor_copy(picked_plane[s][:], tab_plane[:].indirect(lst[:]))
-
-        def permute_weights(s):
+        first_stage(0, 0)
+        first_stage(1, 0)
+        first_stage(0, 1)
+        first_stage(1, 1)
+        for i in range(M // CHUNK, len(chunks)):
             for a in range(PASSES):
-                nc.gpsimd.tensor_copy(
-                    out=w_codes[s][a][:].bitcast(I32).rearrange("p (t b i) -> p t b i", t=PACK, i=8),
-                    in_=w_raw[s][:, a, :].rearrange("p (b t i) -> p t b i", t=PACK, i=8),
-                )
-                if a == 0:
-                    nc.gpsimd.tensor_copy(
-                        out=w_plane[s][:].bitcast(I32).rearrange("p (t b i) -> p t b i", t=PACK, i=2),
-                        in_=w_plane_raw[s][:].bitcast(I32).rearrange("p (b t i) -> p t b i", t=PACK, i=2),
-                    )
+                first_stage(i, a)
 
-        permute_weights(0)
-        permute_weights(1)
-
-        ha_codes = big.tile([P, M], U32, name="ha_codes", offset=4 * T, align_bytes=64)
-        ha_plane = held.tile([P, M], U8, name="ha_plane", align_bytes=64)
-
-        lists = (list_a, list_b)
-        tanh_tiles = {}
-
-        def hidden_sums(s, c):
-            banks = [z_psum.tile([P, PACK, BLOCK], F32, name="z") for h in range(CHUNK // BLOCK - ((s, c) == (0, 0)))]
-            if (s, c) == (0, 0):
-                banks.insert(0, const_psum.tile([P, PACK, BLOCK], F32, name="first_z", tag="fixed"))
-            for a in range(PASSES):
-                words = ring.tile([P, CHUNK], U32, name="picked", align_bytes=64, bufs=5)
-                nc.vector.tensor_copy(
-                    words[:], tab[a][:].bitcast(U32).indirect(lists[s][:, c * CHUNK // 16 : (c + 1) * CHUNK // 16])
-                )
-                for h, z in enumerate(banks):
-                    col = c * CHUNK + h * BLOCK
-                    for t in range(PACK):
-                        nc.tensor.matmul_mx(
-                            out=z[:, t, :],
-                            lhsT=w_codes[s][a][:, t * P : (t + 1) * P].bitcast(FP8X4),
-                            lhsT_scale=w_plane[s][4 * a :, t * P : (t + 1) * P],
-                            rhs=words[:, h * BLOCK : (h + 1) * BLOCK].bitcast(FP8X4),
-                            rhs_scale=picked_plane[s][4 * a :, col : col + BLOCK],
-                            start=(a == 0 and t == 0),
-                            stop=(a == PASSES - 1 and t == PACK - 1),
-                        )
-            th = wide.tile([P, CHUNK, PACK], F32, name="th")
-            for h, z in enumerate(banks):
-                nc.scalar.activation(th[:, h * BLOCK : (h + 1) * BLOCK, :], z[:].rearrange("p t n -> p n t"), ACT.Tanh)
-            tanh_tiles[(s, c)] = th
-
-        def apply_gain(engine, gain, s, col, width, h16):
-            engine.tensor_tensor(
-                out=h16,
-                in0=tanh_tiles[(s, col // CHUNK)][:, col % CHUNK : col % CHUNK + width, :],
-                in1=gain[:, PACK * s : PACK * s + PACK].unsqueeze(1).to_broadcast([P, width, PACK]),
-                op=MULT,
-            )
-
-        def quantise_a(gains, gains_sb):
-            h16 = big.tile([P, M, PACK], BF16, name="ha16", offset=tab_end, align_bytes=64)
-            for col in range(0, M, BLOCK):
-                if col < GPSIMD_COLUMNS:
-                    apply_gain(nc.gpsimd, gains_sb, 0, col, BLOCK, h16[:, col : col + BLOCK, :])
-                else:
-                    apply_gain(nc.vector, gains, 0, col, BLOCK, h16[:, col : col + BLOCK, :])
+        def quantise(h16, width, name, codes):
+            plane = ring.tile([P, width], U8, name=name + "_plane", align_bytes=64)
             nc.vector.quantize_mx(
-                out=ha_codes[:].bitcast(FP8X4), scales=ha_plane[:], in_=h16[:].rearrange("p n t -> p (n t)")
-            )
-
-        def quantise_b(gains, col, width):
-            h16 = ring.tile([P, width, PACK], BF16, name="hb16", align_bytes=64)
-            apply_gain(nc.vector, gains, 1, col, width, h16[:])
-            codes = ring.tile([P, width], U32, name="hb_codes", align_bytes=64)
-            plane = ring.tile([P, width], U8, name="hb_plane", align_bytes=64)
-            nc.vector.quantize_mx(
-                out=codes[:].bitcast(FP8X4), scales=plane[:], in_=h16[:].rearrange("p n t -> p (n t)")
+                out=codes[:].bitcast(FP8X4), scales=plane[:], in_=h16.rearrange("p n t -> p (n t)")
             )
             return codes, plane
+
+        ha = []
+        h16_bytes = 2 * PACK * CHUNK
+        for c in range(M // CHUNK):
+            ha16 = big.tile([P, CHUNK, PACK], BF16, name="ha16_%d" % c, offset=wb_at + c * h16_bytes, align_bytes=64)
+            for h in range(CHUNK // BLOCK):
+                nc.gpsimd.tensor_tensor(
+                    out=ha16[:, h * BLOCK : (h + 1) * BLOCK, :],
+                    in0=tanh_tiles[c][:, h * BLOCK : (h + 1) * BLOCK, :],
+                    in1=gains_a[:],
+                    op=MULT,
+                )
+            if c == 0:
+                codes = big.tile([P, CHUNK], U32, name="ha_codes0", offset=tab_at + 4 * T, align_bytes=64)
+            else:
+                codes = tanhs.tile([P, CHUNK], U32, name="ha_codes1", offset=2 * 4 * PACK * CHUNK, align_bytes=64)
+            ha.append(quantise(ha16[:], CHUNK, "ha", codes))
 
         out_view = out.rearrange("(u p) j -> p u j", p=P)
 
         def scores(col, width, codes, plane):
-            for half in range(2):
-                y = y_psum.tile([P, 2, width], F32, name="y")
+            for half in range(M // CHUNK):
+                y = banks.tile([P, 2, width], F32, name="bank")
                 for v in range(2):
-                    u = 2 * half + v
                     nc.tensor.matmul_mx(
                         out=y[:, v, :],
-                        lhsT=ha_codes[:, u * P : (u + 1) * P].bitcast(FP8X4),
-                        lhsT_scale=ha_plane[:, u * P : (u + 1) * P],
+                        lhsT=ha[half][0][:, v * P : (v + 1) * P].bitcast(FP8X4),
+                        lhsT_scale=ha[half][1][:, v * P : (v + 1) * P],
                         rhs=codes[:].bitcast(FP8X4),
                         rhs_scale=plane[:],
                         start=True,
                         stop=True,
                     )
                 res = wide.tile([P, 2, width], F32, name="res")
-                if col + width == J and half == 1:
+                if col >= J - CHUNK and half == 1:
                     nc.vector.tensor_scalar_mul(res[:], y[:], OUT_SCALE)
                 else:
                     nc.scalar.activation(res[:], y[:], ACT.Copy, scale=OUT_SCALE)
                 nc.sync.dma_start(out=out_view[:, 2 * half : 2 * half + 2, col : col + width], in_=res[:])
 
-        hidden_sums(0, 0)
-        gains = const_psum.tile([P, P], F32, name="gains", tag="fixed")
-        nc.tensor.transpose(gains[:], gain_rows[:], ident[:])
-        gains_sb = held.tile([P, PACK], F32, name="gains_sb")
-        nc.scalar.copy(gains_sb[:], gains[:, 0:PACK])
-        hidden_sums(0, 1)
-        for c in range(J // CHUNK):
-            hidden_sums(1, c)
-        quantise_a(gains, gains_sb)
         last = J // CHUNK - 1
         for c in range(J // CHUNK):
             width = BLOCK if c == last else CHUNK
             for col in range(c * CHUNK, (c + 1) * CHUNK, width):
-                codes, plane = quantise_b(gains, col, width)
+                if c in (1, 2):
+                    hb16 = big.tile(
+                        [P, width, PACK], BF16, name="hb16_%d" % c, offset=wb_at + (c - 1) * h16_bytes, align_bytes=64
+                    )
+                elif c == last:
+                    at = (len(chunks) - 2) * 4 * PACK * CHUNK + col % CHUNK * 2 * PACK
+                    hb16 = tanhs.tile([P, width, PACK], BF16, name="hb16_%d" % col, offset=at, align_bytes=64)
+                else:
+                    hb16 = ring.tile([P, width, PACK], BF16, name="hb16", align_bytes=64)
+                nc.vector.tensor_tensor(
+                    out=hb16[:],
+                    in0=tanh_tiles[M // CHUNK + c][:, col % CHUNK : col % CHUNK + width, :],
+                    in1=gains[:, gain_row[1] : gain_row[1] + PACK].unsqueeze(1).to_broadcast([P, width, PACK]),
+                    op=MULT,
+                )
+                codes = ring.tile([P, width], U32, name="hb_codes", align_bytes=64)
+                codes, plane = quantise(hb16[:], width, "hb", codes)
                 scores(col, width, codes, plane)

@@ -60,12 +60,10 @@ def tile_list_biaff_tanh_none_kernel(
                 out=raw.rearrange("p (a r) -> p a r", a=PASSES), in_=words.rearrange("a p r i -> p a (r i)").bitcast(I32)
             )
 
-        tab_at = R
+        tab_at = 4 * W_RAW
         wb_at = tab_at + PASSES * 4 * T
         nc.vector.memset(tab_plane[:].bitcast(I32), 0)
         nc.sync.dma_start(list_a[:], offs)
-        wa_raw = held.tile([P, W_WORDS], I32, name="wa_raw", align_bytes=64)
-        load_words(wa_raw[:], wa_words)
         load_plane(tab_plane[:].bitcast(I32), tab_scales)
         nc.sync.dma_start(list_b[:], offs2)
 
@@ -85,35 +83,32 @@ def tile_list_biaff_tanh_none_kernel(
         blank = held.tile([P, P], F32, name="blank")
         nc.scalar.activation(blank[:], zeros_late[:], ACT.Tanh)
 
-        wa_plane_raw = big.tile([P, R // 4], I32, name="wa_plane_raw", offset=0, align_bytes=64)
+        wa_raw = big.tile([P, W_RAW], I32, name="wa_raw", offset=0, align_bytes=64)
         wb_raw = big.tile([P, W_RAW], I32, name="wb_raw", offset=wb_at, align_bytes=64)
         raw_words = ((wa_raw[:, 0:R], wa_raw[:, R:W_WORDS]), (wb_raw[:, 0:R], wb_raw[:, R:W_WORDS]))
-        raw_plane = (wa_plane_raw[:], wb_raw[:, W_WORDS:W_RAW])
+        raw_plane = (wa_raw[:, W_WORDS:W_RAW], wb_raw[:, W_WORDS:W_RAW])
         tab = [big.tile([P, T], I32, name="tab%d" % a, offset=tab_at + a * 4 * T, align_bytes=64) for a in range(PASSES)]
 
         def load_table(a):
             nc.sync.dma_start(out=tab[a][:], in_=tab_words[a].rearrange("p t i -> p (t i)").bitcast(I32))
 
+        load_words(wa_raw[:, 0:W_WORDS], wa_words)
         load_table(0)
         nc.gpsimd.memset(raw_plane[0], 0)
-        load_plane(raw_plane[0], wa_scales)
         load_gain(0, sa)
         load_gain(1, sb)
+        load_plane(raw_plane[0], wa_scales)
         load_table(1)
         nc.gpsimd.memset(raw_plane[1], 0)
         load_plane(raw_plane[1], wb_scales)
         for a in range(PASSES):
             nc.sync.dma_start(out=raw_words[1][a], in_=wb_words[a].rearrange("p r i -> p (r i)").bitcast(I32))
 
-        HALF = J // 2
-        picked_plane = {}
-
-        def gather_plane(s, start, tile):
-            nc.vector.tensor_copy(tile[:], tab_plane[:].indirect(lists[s][:, start // 16 : (start + HALF) // 16]))
-            picked_plane[(s, start // HALF)] = tile
-
+        picked_plane = [
+            held.tile([P, n], U8, name="picked_plane%d" % s, align_bytes=64) for s, n in enumerate((M, J))
+        ]
         for s in range(2):
-            gather_plane(s, 0, held.tile([P, HALF], U8, name="picked_plane%d" % s, align_bytes=64))
+            nc.vector.tensor_copy(picked_plane[s][:], tab_plane[:].indirect(lists[s][:]))
 
         for s in range(2):
             for a in range(PASSES):
@@ -141,8 +136,7 @@ def tile_list_biaff_tanh_none_kernel(
         for a in range(PASSES):
             for i in range(AHEAD):
                 gather_words(i, a, a * AHEAD + i)
-        gather_plane(1, HALF, picks.tile([P, HALF], U8, name="picked_plane2", offset=4 * CHUNK * AHEAD, align_bytes=64))
-        freed = [a * AHEAD + i for i in range(1, AHEAD) for a in range(PASSES)][1:]
+        freed = [AHEAD] + [a * AHEAD + i for i in range(1, AHEAD) for a in range(PASSES)][1:]
         for n, (i, a) in enumerate([(i, a) for i in range(AHEAD, len(chunks)) for a in range(PASSES)]):
             gather_words(i, a, freed[n])
 
@@ -161,7 +155,7 @@ def tile_list_biaff_tanh_none_kernel(
                         lhsT=w_codes[s][a][:, t * P : (t + 1) * P].bitcast(FP8X4),
                         lhsT_scale=w_plane[s][4 * a :, t * P : (t + 1) * P],
                         rhs=picked[(i, a)][:, h * BLOCK : (h + 1) * BLOCK].bitcast(FP8X4),
-                        rhs_scale=picked_plane[(s, col // HALF)][4 * a :, col % HALF : col % HALF + BLOCK],
+                        rhs_scale=picked_plane[s][4 * a :, col : col + BLOCK],
                         start=(a == 0 and t == 0),
                         stop=(a == PASSES - 1 and t == PACK - 1),
                     )
@@ -217,7 +211,7 @@ def tile_list_biaff_tanh_none_kernel(
             if c == 0:
                 codes = big.tile([P, CHUNK], U32, name="ha_codes0", offset=tab_at + 4 * T, align_bytes=64)
             else:
-                codes = tanhs.tile([P, CHUNK], U32, name="ha_codes1", offset=2 * 4 * PACK * CHUNK, align_bytes=64)
+                codes = tanhs.tile([P, CHUNK], U32, name="ha_codes1", offset=3 * 4 * PACK * CHUNK, align_bytes=64)
             ha.append(quantise(ha16[:], CHUNK, "ha", codes))
 
         out_view = out.rearrange("(u p) j -> p u j", p=P)
@@ -246,7 +240,7 @@ def tile_list_biaff_tanh_none_kernel(
         for c in range(J // CHUNK):
             width = BLOCK if c == last else CHUNK
             for col in range(c * CHUNK, (c + 1) * CHUNK, width):
-                if c in (1, 2):
+                if c == 2:
                     hb16 = big.tile(
                         [P, width, PACK], BF16, name="hb16_%d" % c, offset=wb_at + (c - 1) * h16_bytes, align_bytes=64
                     )

@@ -190,71 +190,81 @@ def tile_list_biaff_tanh_none_kernel(
             for a in range(PASSES):
                 first_stage(i, a)
 
-        def quantise(h16, width, name, codes):
-            plane = ring.tile([P, width], U8, name=name + "_plane", align_bytes=64)
+        th_bytes = 4 * PACK * CHUNK
+        h16_bytes = 2 * PACK * CHUNK
+
+        def quantise(h16, codes):
+            plane = ring.tile([P, codes.shape[1]], U8, name="h_plane", align_bytes=64, bufs=8)
             nc.vector.quantize_mx(
-                out=codes[:].bitcast(FP8X4), scales=plane[:], in_=h16.rearrange("p n t -> p (n t)")
+                out=codes[:].bitcast(FP8X4), scales=plane[:], in_=h16[:].rearrange("p n t -> p (n t)")
             )
             return codes, plane
 
-        ha = []
-        h16_bytes = 2 * PACK * CHUNK
+        ha16 = []
         for c in range(M // CHUNK):
-            ha16 = big.tile([P, CHUNK, PACK], BF16, name="ha16_%d" % c, offset=wb_at + c * h16_bytes, align_bytes=64)
+            h16 = big.tile([P, CHUNK, PACK], BF16, name="ha16_%d" % c, offset=wb_at + c * h16_bytes, align_bytes=64)
             for h in range(CHUNK // BLOCK):
                 nc.gpsimd.tensor_tensor(
-                    out=ha16[:, h * BLOCK : (h + 1) * BLOCK, :],
+                    out=h16[:, h * BLOCK : (h + 1) * BLOCK, :],
                     in0=tanh_tiles[c][:, h * BLOCK : (h + 1) * BLOCK, :],
                     in1=gains_a[:],
                     op=MULT,
                 )
-            if c == 0:
-                codes = big.tile([P, CHUNK], U32, name="ha_codes0", offset=tab_at + 4 * T, align_bytes=64)
-            else:
-                codes = tanhs.tile([P, CHUNK], U32, name="ha_codes1", offset=3 * 4 * PACK * CHUNK, align_bytes=64)
-            ha.append(quantise(ha16[:], CHUNK, "ha", codes))
+            ha16.append(h16)
+
+        def scale_b(col, h16):
+            width = h16.shape[1]
+            nc.vector.tensor_tensor(
+                out=h16[:],
+                in0=tanh_tiles[M // CHUNK + col // CHUNK][:, col % CHUNK : col % CHUNK + width, :],
+                in1=gains[:, gain_row[1] : gain_row[1] + PACK].unsqueeze(1).to_broadcast([P, width, PACK]),
+                op=MULT,
+            )
+            return h16
 
         out_view = out.rearrange("(u p) j -> p u j", p=P)
 
-        def scores(col, width, codes, plane):
-            for half in range(M // CHUNK):
-                y = banks.tile([P, 2, width], F32, name="bank")
-                for v in range(2):
-                    nc.tensor.matmul_mx(
-                        out=y[:, v, :],
-                        lhsT=ha[half][0][:, v * P : (v + 1) * P].bitcast(FP8X4),
-                        lhsT_scale=ha[half][1][:, v * P : (v + 1) * P],
-                        rhs=codes[:].bitcast(FP8X4),
-                        rhs_scale=plane[:],
-                        start=True,
-                        stop=True,
-                    )
-                res = wide.tile([P, 2, width], F32, name="res")
-                if col >= J - CHUNK and half == 1:
-                    nc.vector.tensor_scalar_mul(res[:], y[:], OUT_SCALE)
-                else:
-                    nc.scalar.activation(res[:], y[:], ACT.Copy, scale=OUT_SCALE)
-                nc.sync.dma_start(out=out_view[:, 2 * half : 2 * half + 2, col : col + width], in_=res[:])
-
-        last = J // CHUNK - 1
-        for c in range(J // CHUNK):
-            width = BLOCK if c == last else CHUNK
-            for col in range(c * CHUNK, (c + 1) * CHUNK, width):
-                if c == 2:
-                    hb16 = big.tile(
-                        [P, width, PACK], BF16, name="hb16_%d" % c, offset=wb_at + (c - 1) * h16_bytes, align_bytes=64
-                    )
-                elif c == last:
-                    at = (len(chunks) - 2) * 4 * PACK * CHUNK + col % CHUNK * 2 * PACK
-                    hb16 = tanhs.tile([P, width, PACK], BF16, name="hb16_%d" % col, offset=at, align_bytes=64)
-                else:
-                    hb16 = ring.tile([P, width, PACK], BF16, name="hb16", align_bytes=64)
-                nc.vector.tensor_tensor(
-                    out=hb16[:],
-                    in0=tanh_tiles[M // CHUNK + c][:, col % CHUNK : col % CHUNK + width, :],
-                    in1=gains[:, gain_row[1] : gain_row[1] + PACK].unsqueeze(1).to_broadcast([P, width, PACK]),
-                    op=MULT,
+        def scores(col, row_tiles, hb, on_vector=False):
+            width = hb[0].shape[1]
+            y = banks.tile([P, len(row_tiles), width], F32, name="bank")
+            for n, u in enumerate(row_tiles):
+                codes, plane = ha[u // 2]
+                nc.tensor.matmul_mx(
+                    out=y[:, n, :],
+                    lhsT=codes[:, u % 2 * P : (u % 2 + 1) * P].bitcast(FP8X4),
+                    lhsT_scale=plane[:, u % 2 * P : (u % 2 + 1) * P],
+                    rhs=hb[0][:].bitcast(FP8X4),
+                    rhs_scale=hb[1][:],
+                    start=True,
+                    stop=True,
                 )
-                codes = ring.tile([P, width], U32, name="hb_codes", align_bytes=64)
-                codes, plane = quantise(hb16[:], width, "hb", codes)
-                scores(col, width, codes, plane)
+            res = wide.tile([P, len(row_tiles), width], F32, name="res")
+            if on_vector:
+                nc.vector.tensor_scalar_mul(res[:], y[:], OUT_SCALE)
+            else:
+                nc.scalar.activation(res[:], y[:], ACT.Copy, scale=OUT_SCALE)
+            nc.sync.dma_start(out=out_view[:, row_tiles[0] : row_tiles[-1] + 1, col : col + width], in_=res[:])
+
+        def codes_after_second_product(n):
+            at = (M // CHUNK + 1) * th_bytes + n * 4 * CHUNK
+            return tanhs.tile([P, CHUNK], U32, name="h_codes%d" % n, offset=at, align_bytes=64)
+
+        hb16 = [scale_b(c * CHUNK, ring.tile([P, CHUNK, PACK], BF16, name="hb16", align_bytes=64)) for c in range(2)]
+        ha = [quantise(ha16[0], codes_after_second_product(0))]
+        hb = quantise(hb16[0], codes_after_second_product(1))
+        scores(0, (0, 1), hb)
+        ha.append(quantise(ha16[1], codes_after_second_product(2)))
+        scores(0, (2, 3), hb)
+        hb = quantise(hb16[1], codes_after_second_product(3))
+        scores(CHUNK, (0, 1), hb)
+        scores(CHUNK, (2, 3), hb)
+
+        late16 = big.tile([P, J // 2, PACK], BF16, name="late16", offset=wb_at - h16_bytes, align_bytes=64)
+        for col in range(J // 2, J, BLOCK):
+            h16 = scale_b(col, late16[:, col - J // 2 : col - J // 2 + BLOCK, :])
+            hb = quantise(h16, ring.tile([P, BLOCK], U32, name="hb_codes", align_bytes=64))
+            if col < J - CHUNK:
+                scores(col, (0, 1, 2, 3), hb)
+            else:
+                scores(col, (0, 1), hb)
+                scores(col, (2, 3), hb, on_vector=True)

@@ -224,7 +224,7 @@ def tile_list_biaff_tanh_none_kernel(
 
         out_view = out.rearrange("(u p) j -> p u j", p=P)
 
-        def scores(col, row_tiles, hb, on_vector=False):
+        def scores(row_tiles, hb, res, on_vector=False):
             width = hb[0].shape[1]
             y = banks.tile([P, len(row_tiles), width], F32, name="bank")
             for n, u in enumerate(row_tiles):
@@ -238,12 +238,18 @@ def tile_list_biaff_tanh_none_kernel(
                     start=True,
                     stop=True,
                 )
-            res = wide.tile([P, len(row_tiles), width], F32, name="res")
             if on_vector:
-                nc.vector.tensor_scalar_mul(res[:], y[:], OUT_SCALE)
+                nc.vector.tensor_scalar_mul(res, y[:], OUT_SCALE)
             else:
-                nc.scalar.activation(res[:], y[:], ACT.Copy, scale=OUT_SCALE)
-            nc.sync.dma_start(out=out_view[:, row_tiles[0] : row_tiles[-1] + 1, col : col + width], in_=res[:])
+                nc.scalar.activation(res, y[:], ACT.Copy, scale=OUT_SCALE)
+
+        def store(c, row_tiles, res):
+            nc.sync.dma_start(out=out_view[:, row_tiles[0] : row_tiles[-1] + 1, c * CHUNK : (c + 1) * CHUNK], in_=res)
+
+        def scores_of_chunk(c, row_tiles, hb):
+            res = wide.tile([P, 2, CHUNK], F32, name="res")
+            scores(row_tiles, hb, res[:])
+            store(c, row_tiles, res[:])
 
         def codes_after_second_product(n):
             at = (M // CHUNK + 1) * th_bytes + n * 4 * CHUNK
@@ -252,19 +258,22 @@ def tile_list_biaff_tanh_none_kernel(
         hb16 = [scale_b(c * CHUNK, ring.tile([P, CHUNK, PACK], BF16, name="hb16", align_bytes=64)) for c in range(2)]
         ha = [quantise(ha16[0], codes_after_second_product(0))]
         hb = quantise(hb16[0], codes_after_second_product(1))
-        scores(0, (0, 1), hb)
+        scores_of_chunk(0, (0, 1), hb)
         ha.append(quantise(ha16[1], codes_after_second_product(2)))
-        scores(0, (2, 3), hb)
+        scores_of_chunk(0, (2, 3), hb)
         hb = quantise(hb16[1], codes_after_second_product(3))
-        scores(CHUNK, (0, 1), hb)
-        scores(CHUNK, (2, 3), hb)
+        scores_of_chunk(1, (0, 1), hb)
+        scores_of_chunk(1, (2, 3), hb)
 
         late16 = big.tile([P, J // 2, PACK], BF16, name="late16", offset=wb_at - h16_bytes, align_bytes=64)
-        for col in range(J // 2, J, BLOCK):
-            h16 = scale_b(col, late16[:, col - J // 2 : col - J // 2 + BLOCK, :])
-            hb = quantise(h16, ring.tile([P, BLOCK], U32, name="hb_codes", align_bytes=64))
-            if col < J - CHUNK:
-                scores(col, (0, 1, 2, 3), hb)
-            else:
-                scores(col, (0, 1), hb)
-                scores(col, (2, 3), hb, on_vector=True)
+        for c in (2, 3):
+            groups = [(0, 1, 2, 3)] if c == 2 else [(0, 1), (2, 3)]
+            res = [held.tile([P, len(g), CHUNK], F32, name="res%d%d" % (c, g[0])) for g in groups]
+            for first in range(0, CHUNK, BLOCK):
+                col = c * CHUNK + first
+                h16 = scale_b(col, late16[:, col - J // 2 : col - J // 2 + BLOCK, :])
+                hb = quantise(h16, ring.tile([P, BLOCK], U32, name="hb_codes", align_bytes=64))
+                for n, g in enumerate(groups):
+                    scores(g, hb, res[n][:, :, first : first + BLOCK], on_vector=(n == 1))
+            for n, g in enumerate(groups):
+                store(c, g, res[n][:])

@@ -51,8 +51,8 @@ def tile_list_biaff_tanh_none_kernel(
         ]
         gain_rows = held.tile([P, P], F32, name="gain_rows")
 
-        def load_plane(plane, scales):
-            for q in range(4):
+        def load_plane(plane, scales, quadrants=range(4)):
+            for q in quadrants:
                 nc.sync.dma_start(out=plane[32 * q : 32 * q + 8, :], in_=scales[:, 4 * q : 4 * q + 4, :].bitcast(I32))
 
         def load_words(raw, words):
@@ -64,7 +64,13 @@ def tile_list_biaff_tanh_none_kernel(
         wb_at = tab_at + PASSES * 4 * T
         nc.vector.memset(tab_plane[:].bitcast(I32), 0)
         nc.sync.dma_start(list_a[:], offs)
-        load_plane(tab_plane[:].bitcast(I32), tab_scales)
+        for a in range(PASSES):
+            for q in (1, 3):
+                nc.sync.dma_start(
+                    out=tab_plane[:].bitcast(I32)[32 * q + 4 * a : 32 * q + 4 * a + 4, :],
+                    in_=tab_scales[a, 4 * q : 4 * q + 4, :].bitcast(I32),
+                )
+        load_plane(tab_plane[:].bitcast(I32), tab_scales, (0, 2))
         nc.sync.dma_start(list_b[:], offs2)
 
         gain_row = (0, PACK)

@@ -64,13 +64,13 @@ def tile_list_biaff_tanh_none_kernel(
         wb_at = tab_at + PASSES * 4 * T
         nc.vector.memset(tab_plane[:].bitcast(I32), 0)
         nc.sync.dma_start(list_a[:], offs)
+        load_plane(tab_plane[:].bitcast(I32), tab_scales, (0, 2))
         for a in range(PASSES):
             for q in (1, 3):
                 nc.sync.dma_start(
                     out=tab_plane[:].bitcast(I32)[32 * q + 4 * a : 32 * q + 4 * a + 4, :],
                     in_=tab_scales[a, 4 * q : 4 * q + 4, :].bitcast(I32),
                 )
-        load_plane(tab_plane[:].bitcast(I32), tab_scales, (0, 2))
         nc.sync.dma_start(list_b[:], offs2)
 
         gain_row = (0, PACK)
@@ -151,26 +151,27 @@ def tile_list_biaff_tanh_none_kernel(
 
         def first_stage(i, a):
             s, c = chunks[i]
-            for h in range(CHUNK // BLOCK):
+            width = BLOCK if s == 0 else CHUNK
+            places = PACK * BLOCK // width
+            for h in range(2):
                 if a == 0:
-                    sums[(i, h)] = banks.tile([P, PACK, BLOCK], F32, name="bank")
-                col = c * CHUNK + h * BLOCK
-                for t in range(PACK):
+                    sums[(i, h)] = banks.tile([P, places, width], F32, name="bank")
+                first = h * BLOCK if s == 0 else 0
+                for n in range(places):
+                    t = n if s == 0 else h * places + n
                     nc.tensor.matmul_mx(
-                        out=sums[(i, h)][:, t, :],
+                        out=sums[(i, h)][:, n, :],
                         lhsT=w_codes[s][a][:, t * P : (t + 1) * P].bitcast(FP8X4),
                         lhsT_scale=w_plane[s][4 * a :, t * P : (t + 1) * P],
-                        rhs=picked[(i, a)][:, h * BLOCK : (h + 1) * BLOCK].bitcast(FP8X4),
-                        rhs_scale=picked_plane[s][4 * a :, col : col + BLOCK],
-                        start=(a == 0 and t == 0),
-                        stop=(a == PASSES - 1 and t == PACK - 1),
+                        rhs=picked[(i, a)][:, first : first + width].bitcast(FP8X4),
+                        rhs_scale=picked_plane[s][4 * a :, c * CHUNK + first : c * CHUNK + first + width],
+                        start=(a == 0 and n == 0),
+                        stop=(a == PASSES - 1 and n == places - 1),
                     )
             if a == PASSES - 1:
-                th = tanhs.tile([P, CHUNK, PACK], F32, name="th%d" % i, offset=i * 4 * PACK * CHUNK, align_bytes=64)
-                for h in range(CHUNK // BLOCK):
-                    nc.scalar.activation(
-                        th[:, h * BLOCK : (h + 1) * BLOCK, :], sums[(i, h)][:].rearrange("p t n -> p n t"), ACT.Tanh
-                    )
+                th = tanhs.tile([P, 2, width, places], F32, name="th%d" % i, offset=i * 4 * PACK * CHUNK, align_bytes=64)
+                for h in range(2):
+                    nc.scalar.activation(th[:, h, :, :], sums[(i, h)][:].rearrange("p t n -> p n t"), ACT.Tanh)
                 tanh_tiles[i] = th
 
         ident = held.tile([P, P], F32, name="ident")
@@ -212,7 +213,7 @@ def tile_list_biaff_tanh_none_kernel(
             for h in range(CHUNK // BLOCK):
                 nc.gpsimd.tensor_tensor(
                     out=h16[:, h * BLOCK : (h + 1) * BLOCK, :],
-                    in0=tanh_tiles[c][:, h * BLOCK : (h + 1) * BLOCK, :],
+                    in0=tanh_tiles[c][:, h, :, :],
                     in1=gains_a[:],
                     op=MULT,
                 )
@@ -221,9 +222,14 @@ def tile_list_biaff_tanh_none_kernel(
         def scale_b(col, h16):
             width = h16.shape[1]
             nc.vector.tensor_tensor(
-                out=h16[:],
-                in0=tanh_tiles[M // CHUNK + col // CHUNK][:, col % CHUNK : col % CHUNK + width, :],
-                in1=gains[:, gain_row[1] : gain_row[1] + PACK].unsqueeze(1).to_broadcast([P, width, PACK]),
+                out=h16[:].rearrange("p n (u e) -> p n u e", e=2),
+                in0=tanh_tiles[M // CHUNK + col // CHUNK][:, :, col % CHUNK : col % CHUNK + width, :].rearrange(
+                    "p u n e -> p n u e"
+                ),
+                in1=gains[:, gain_row[1] : gain_row[1] + PACK]
+                .rearrange("p (u e) -> p u e", e=2)
+                .unsqueeze(1)
+                .to_broadcast([P, width, 2, 2]),
                 op=MULT,
             )
             return h16

@@ -200,12 +200,8 @@ def tile_list_biaff_tanh_none_kernel(
         th_bytes = 4 * PACK * CHUNK
         h16_bytes = 2 * PACK * CHUNK
 
-        def quantise(h16, codes):
-            plane = ring.tile([P, codes.shape[1]], U8, name="h_plane", align_bytes=64, bufs=8)
-            nc.vector.quantize_mx(
-                out=codes[:].bitcast(FP8X4), scales=plane[:], in_=h16[:].rearrange("p n t -> p (n t)")
-            )
-            return codes, plane
+        def quantise(h16, codes, plane):
+            nc.vector.quantize_mx(out=codes.bitcast(FP8X4), scales=plane, in_=h16.rearrange("p n t -> p (n t)"))
 
         ha16 = []
         for c in range(M // CHUNK):
@@ -236,17 +232,18 @@ def tile_list_biaff_tanh_none_kernel(
 
         out_view = out.rearrange("(u p) j -> p u j", p=P)
 
-        def scores(row_tiles, hb, res, on_vector=False):
-            width = hb[0].shape[1]
-            y = banks.tile([P, len(row_tiles), width], F32, name="bank")
+        first_codes = tanhs.tile([P, M + J // 2], U32, name="first_codes", offset=(M // CHUNK + 1) * th_bytes, align_bytes=64)
+        first_plane = held.tile([P, M + J // 2], U8, name="first_plane", align_bytes=64)
+
+        def scores(row_tiles, codes, plane, res, on_vector=False):
+            y = banks.tile([P, len(row_tiles), codes.shape[1]], F32, name="bank")
             for n, u in enumerate(row_tiles):
-                codes, plane = ha[u // 2]
                 nc.tensor.matmul_mx(
                     out=y[:, n, :],
-                    lhsT=codes[:, u % 2 * P : (u % 2 + 1) * P].bitcast(FP8X4),
-                    lhsT_scale=plane[:, u % 2 * P : (u % 2 + 1) * P],
-                    rhs=hb[0][:].bitcast(FP8X4),
-                    rhs_scale=hb[1][:],
+                    lhsT=first_codes[:, u * P : (u + 1) * P].bitcast(FP8X4),
+                    lhsT_scale=first_plane[:, u * P : (u + 1) * P],
+                    rhs=codes.bitcast(FP8X4),
+                    rhs_scale=plane,
                     start=True,
                     stop=True,
                 )
@@ -255,37 +252,41 @@ def tile_list_biaff_tanh_none_kernel(
             else:
                 nc.scalar.activation(res, y[:], ACT.Copy, scale=OUT_SCALE)
 
-        def store(c, row_tiles, res):
-            nc.sync.dma_start(out=out_view[:, row_tiles[0] : row_tiles[-1] + 1, c * CHUNK : (c + 1) * CHUNK], in_=res)
+        def store(row_tiles, col, res):
+            nc.sync.dma_start(out=out_view[:, row_tiles[0] : row_tiles[-1] + 1, col : col + res.shape[2]], in_=res)
 
-        def scores_of_chunk(c, row_tiles, hb):
-            res = wide.tile([P, 2, CHUNK], F32, name="res")
-            scores(row_tiles, hb, res[:])
-            store(c, row_tiles, res[:])
+        def quantise_first(h16, at):
+            quantise(h16, first_codes[:, at : at + h16.shape[1]], first_plane[:, at : at + h16.shape[1]])
 
-        def codes_after_second_product(n):
-            at = (M // CHUNK + 1) * th_bytes + n * 4 * CHUNK
-            return tanhs.tile([P, CHUNK], U32, name="h_codes%d" % n, offset=at, align_bytes=64)
+        def first_scores(row_tiles, col, width):
+            res = wide.tile([P, len(row_tiles), width], F32, name="res")
+            cols = slice(M + col, M + col + width)
+            scores(row_tiles, first_codes[:, cols], first_plane[:, cols], res[:])
+            store(row_tiles, col, res[:])
 
         hb16 = [scale_b(c * CHUNK, ring.tile([P, CHUNK, PACK], BF16, name="hb16", align_bytes=64)) for c in range(2)]
-        ha = [quantise(ha16[0], codes_after_second_product(0))]
-        hb = quantise(hb16[0], codes_after_second_product(1))
-        scores_of_chunk(0, (0, 1), hb)
-        ha.append(quantise(ha16[1], codes_after_second_product(2)))
-        scores_of_chunk(0, (2, 3), hb)
-        hb = quantise(hb16[1], codes_after_second_product(3))
-        scores_of_chunk(1, (0, 1), hb)
-        scores_of_chunk(1, (2, 3), hb)
+        quantise_first(ha16[0][:, 0:BLOCK, :], 0)
+        quantise_first(hb16[0][:], M)
+        first_scores((0,), 0, CHUNK)
+        quantise_first(ha16[0][:, BLOCK:CHUNK, :], BLOCK)
+        first_scores((1,), 0, CHUNK)
+        quantise_first(hb16[1][:], M + CHUNK)
+        first_scores((0, 1), CHUNK, CHUNK)
+        quantise_first(ha16[1][:], CHUNK)
+        first_scores((2,), 0, 2 * CHUNK)
+        first_scores((3,), 0, 2 * CHUNK)
 
         late16 = big.tile([P, J // 2, PACK], BF16, name="late16", offset=wb_at - h16_bytes, align_bytes=64)
+        halves = ((0, 1), (2, 3))
         for c in (2, 3):
-            groups = [(0, 1, 2, 3)] if c == 2 else [(0, 1), (2, 3)]
-            res = [held.tile([P, len(g), CHUNK], F32, name="res%d%d" % (c, g[0])) for g in groups]
+            res = [wide.tile([P, 2, CHUNK], F32, name="res") for half in halves]
             for first in range(0, CHUNK, BLOCK):
                 col = c * CHUNK + first
                 h16 = scale_b(col, late16[:, col - J // 2 : col - J // 2 + BLOCK, :])
-                hb = quantise(h16, ring.tile([P, BLOCK], U32, name="hb_codes", align_bytes=64))
-                for n, g in enumerate(groups):
-                    scores(g, hb, res[n][:, :, first : first + BLOCK], on_vector=(n == 1))
-            for n, g in enumerate(groups):
-                store(c, g, res[n][:])
+                codes = ring.tile([P, BLOCK], U32, name="hb_codes", align_bytes=64)
+                plane = ring.tile([P, BLOCK], U8, name="hb_plane", align_bytes=64)
+                quantise(h16, codes[:], plane[:])
+                for n, half in enumerate(halves):
+                    scores(half, codes[:], plane[:], res[n][:, :, first : first + BLOCK], on_vector=(c == 3 and n == 1))
+            for n, half in enumerate(halves):
+                store(half, c * CHUNK, res[n][:])

@@ -86,8 +86,17 @@ def tile_list_biaff_tanh_none_kernel(
         nc.gpsimd.tensor_copy(gain_rows[:], zeros_early[:])
         zeros_late = big.tile([P, P], F32, name="zeros_late", offset=wb_at - 2 * P)
         nc.vector.memset(zeros_late[:], 0.0)
-        blank = held.tile([P, P], F32, name="blank")
-        nc.scalar.activation(blank[:], zeros_late[:], ACT.Tanh)
+
+        ident = held.tile([P, P], F32, name="ident")
+        nc.gpsimd.affine_select(
+            out=ident[:],
+            in_=zeros_late[:],
+            compare_op=mybir.AluOpType.not_equal,
+            fill=1.0,
+            base=0,
+            pattern=[[-1, P]],
+            channel_multiplier=1,
+        )
 
         wa_raw = big.tile([P, W_RAW], I32, name="wa_raw", offset=0, align_bytes=64)
         wb_raw = big.tile([P, W_RAW], I32, name="wb_raw", offset=wb_at, align_bytes=64)
@@ -174,16 +183,6 @@ def tile_list_biaff_tanh_none_kernel(
                     nc.scalar.activation(th[:, h, :, :], sums[(i, h)][:].rearrange("p t n -> p n t"), ACT.Tanh)
                 tanh_tiles[i] = th
 
-        ident = held.tile([P, P], F32, name="ident")
-        nc.gpsimd.affine_select(
-            out=ident[:],
-            in_=blank[:],
-            compare_op=mybir.AluOpType.not_equal,
-            fill=1.0,
-            base=0,
-            pattern=[[-1, P]],
-            channel_multiplier=1,
-        )
         gains = const_psum.tile([P, P], F32, name="gains")
         nc.tensor.transpose(gains[:], gain_rows[:], ident[:])
         gains_a = held.tile([P, BLOCK, PACK], F32, name="gains_a")

@@ -24,6 +24,7 @@ OUT_SCALE = 0.03125
 W_WORDS = PASSES * R
 W_RAW = W_WORDS + R // 4
 AHEAD = 4
+ON_SCALAR = 64
 
 
 def tile_list_biaff_tanh_none_kernel(
@@ -187,6 +188,9 @@ def tile_list_biaff_tanh_none_kernel(
         nc.tensor.transpose(gains[:], gain_rows[:], ident[:])
         gains_a = held.tile([P, BLOCK, PACK], F32, name="gains_a")
         nc.scalar.copy(gains_a[:], gains[:, gain_row[0] : gain_row[0] + PACK].unsqueeze(1).to_broadcast([P, BLOCK, PACK]))
+        gains_b = held.tile([P, PACK], F32, name="gains_b")
+        nc.scalar.copy(gains_b[:], gains[:, gain_row[1] : gain_row[1] + PACK])
+        hb16 = [ring.tile([P, CHUNK, PACK], BF16, name="hb16", align_bytes=64) for c in range(2)]
 
         first_stage(0, 0)
         first_stage(1, 0)
@@ -195,6 +199,13 @@ def tile_list_biaff_tanh_none_kernel(
         for i in range(M // CHUNK, len(chunks)):
             for a in range(PASSES):
                 first_stage(i, a)
+            if i == M // CHUNK + 1:
+                by_place = held.tile([P, PACK, ON_SCALAR], BF16, name="by_place", align_bytes=64)
+                for t in range(PACK):
+                    nc.scalar.activation(
+                        by_place[:, t, :], tanh_tiles[i][:, t // 2, 0:ON_SCALAR, t % 2], ACT.Copy, scale=gains_b[:, t : t + 1]
+                    )
+                nc.scalar.copy(hb16[1][:, 0:ON_SCALAR, :], by_place[:].rearrange("p t n -> p n t"))
 
         th_bytes = 4 * PACK * CHUNK
         h16_bytes = 2 * PACK * CHUNK
@@ -205,11 +216,12 @@ def tile_list_biaff_tanh_none_kernel(
         ha16 = []
         for c in range(M // CHUNK):
             h16 = big.tile([P, CHUNK, PACK], BF16, name="ha16_%d" % c, offset=wb_at + c * h16_bytes, align_bytes=64)
-            for h in range(CHUNK // BLOCK):
+            step = c + 1
+            for h in range(0, CHUNK // BLOCK, step):
                 nc.gpsimd.tensor_tensor(
-                    out=h16[:, h * BLOCK : (h + 1) * BLOCK, :],
-                    in0=tanh_tiles[c][:, h, :, :],
-                    in1=gains_a[:],
+                    out=h16[:, h * BLOCK : (h + step) * BLOCK, :].rearrange("p (h n) t -> p h (n t)", h=step),
+                    in0=tanh_tiles[c][:, h : h + step, :, :].rearrange("p h n t -> p h (n t)"),
+                    in1=gains_a[:].rearrange("p n t -> p (n t)").unsqueeze(1).to_broadcast([P, step, BLOCK * PACK]),
                     op=MULT,
                 )
             ha16.append(h16)
@@ -263,7 +275,8 @@ def tile_list_biaff_tanh_none_kernel(
             scores(row_tiles, first_codes[:, cols], first_plane[:, cols], res[:])
             store(row_tiles, col, res[:])
 
-        hb16 = [scale_b(c * CHUNK, ring.tile([P, CHUNK, PACK], BF16, name="hb16", align_bytes=64)) for c in range(2)]
+        scale_b(0, hb16[0])
+        scale_b(CHUNK + ON_SCALAR, hb16[1][:, ON_SCALAR:, :])
         quantise_first(ha16[0][:, 0:BLOCK, :], 0)
         quantise_first(hb16[0][:], M)
         first_scores((0,), 0, CHUNK)

@@ -24,7 +24,8 @@ OUT_SCALE = 0.03125
 W_WORDS = PASSES * R
 W_RAW = W_WORDS + R // 4
 AHEAD = 4
-ON_SCALAR = 64
+ON_SCALAR = 48
+EARLY = 160
 
 
 def tile_list_biaff_tanh_none_kernel(
@@ -157,6 +158,7 @@ def tile_list_biaff_tanh_none_kernel(
             gather_words(i, a, freed[n])
 
         tanh_tiles = {}
+        split_chunk = M // CHUNK + 1
         sums = {}
 
         def first_stage(i, a):
@@ -178,7 +180,16 @@ def tile_list_biaff_tanh_none_kernel(
                         start=(a == 0 and n == 0),
                         stop=(a == PASSES - 1 and n == places - 1),
                     )
-            if a == PASSES - 1:
+            if a == PASSES - 1 and i == split_chunk:
+                at = i * 4 * PACK * CHUNK
+                early = tanhs.tile([P, 2, EARLY, 2], F32, name="th_early", offset=at, align_bytes=64)
+                rest = tanhs.tile([P, 2, CHUNK - EARLY, 2], F32, name="th_rest", offset=at + 4 * PACK * EARLY, align_bytes=64)
+                for h in range(2):
+                    nc.scalar.activation(early[:, h, :, :], sums[(i, h)][:, :, :EARLY].rearrange("p t n -> p n t"), ACT.Tanh)
+                    nc.scalar.activation(rest[:, h, :, :], sums[(i, h)][:, :, EARLY:].rearrange("p t n -> p n t"), ACT.Tanh)
+                tanh_tiles[i] = early
+                tanh_tiles["rest"] = rest
+            elif a == PASSES - 1:
                 th = tanhs.tile([P, 2, width, places], F32, name="th%d" % i, offset=i * 4 * PACK * CHUNK, align_bytes=64)
                 for h in range(2):
                     nc.scalar.activation(th[:, h, :, :], sums[(i, h)][:].rearrange("p t n -> p n t"), ACT.Tanh)
@@ -228,11 +239,13 @@ def tile_list_biaff_tanh_none_kernel(
 
         def scale_b(col, h16):
             width = h16.shape[1]
+            if col == CHUNK + EARLY:
+                th = tanh_tiles["rest"][:]
+            else:
+                th = tanh_tiles[M // CHUNK + col // CHUNK][:, :, col % CHUNK : col % CHUNK + width, :]
             nc.vector.tensor_tensor(
                 out=h16[:].rearrange("p n (u e) -> p n u e", e=2),
-                in0=tanh_tiles[M // CHUNK + col // CHUNK][:, :, col % CHUNK : col % CHUNK + width, :].rearrange(
-                    "p u n e -> p n u e"
-                ),
+                in0=th.rearrange("p u n e -> p n u e"),
                 in1=gains[:, gain_row[1] : gain_row[1] + PACK]
                 .rearrange("p (u e) -> p u e", e=2)
                 .unsqueeze(1)
@@ -243,7 +256,7 @@ def tile_list_biaff_tanh_none_kernel(
 
         out_view = out.rearrange("(u p) j -> p u j", p=P)
 
-        first_codes = tanhs.tile([P, M + J // 2], U32, name="first_codes", offset=(M // CHUNK + 1) * th_bytes, align_bytes=64)
+        first_codes = tanhs.tile([P, M + J // 2], U32, name="first_codes", offset=split_chunk * th_bytes - th_bytes // 2, align_bytes=64)
         first_plane = held.tile([P, M + J // 2], U8, name="first_plane", align_bytes=64)
 
         def scores(row_tiles, codes, plane, res, on_vector=False):
@@ -276,7 +289,8 @@ def tile_list_biaff_tanh_none_kernel(
             store(row_tiles, col, res[:])
 
         scale_b(0, hb16[0])
-        scale_b(CHUNK + ON_SCALAR, hb16[1][:, ON_SCALAR:, :])
+        scale_b(CHUNK + ON_SCALAR, hb16[1][:, ON_SCALAR:EARLY, :])
+        scale_b(CHUNK + EARLY, hb16[1][:, EARLY:, :])
         quantise_first(ha16[0][:, 0:BLOCK, :], 0)
         quantise_first(hb16[0][:], M)
         first_scores((0,), 0, CHUNK)
@@ -292,13 +306,17 @@ def tile_list_biaff_tanh_none_kernel(
         halves = ((0, 1), (2, 3))
         for c in (2, 3):
             res = [wide.tile([P, 2, CHUNK], F32, name="res") for half in halves]
+            blocks = []
             for first in range(0, CHUNK, BLOCK):
                 col = c * CHUNK + first
                 h16 = scale_b(col, late16[:, col - J // 2 : col - J // 2 + BLOCK, :])
                 codes = ring.tile([P, BLOCK], U32, name="hb_codes", align_bytes=64)
                 plane = ring.tile([P, BLOCK], U8, name="hb_plane", align_bytes=64)
                 quantise(h16, codes[:], plane[:])
-                for n, half in enumerate(halves):
-                    scores(half, codes[:], plane[:], res[n][:, :, first : first + BLOCK], on_vector=(c == 3 and n == 1))
-            for n, half in enumerate(halves):
-                store(half, c * CHUNK, res[n][:])
+                blocks.append((first, codes, plane))
+            order = [(n, k) for n in range(2) for k in range(2)] if c == 2 else [(n, k) for k in range(2) for n in range(2)]
+            for n, k in order:
+                first, codes, plane = blocks[k]
+                scores(halves[n], codes[:], plane[:], res[n][:, :, first : first + BLOCK], on_vector=(c == 3 and n == 1))
+                if k == 1:
+                    store(halves[n], c * CHUNK, res[n][:])

@@ -51,7 +51,8 @@ def tile_list_biaff_tanh_none_kernel(
             [held.tile([P, R], U32, name="w_codes%d%d" % (s, a), align_bytes=64) for a in range(PASSES)]
             for s in range(2)
         ]
-        gain_rows = held.tile([P, P], F32, name="gain_rows")
+        gain_rows = held.tile([P, R], F32, name="gain_rows")
+        gain_by_place = held.tile([P, PACK, P], F32, name="gain_by_place")
 
         def load_plane(plane, scales, quadrants=range(4)):
             for q in quadrants:
@@ -75,17 +76,14 @@ def tile_list_biaff_tanh_none_kernel(
                 )
         nc.sync.dma_start(list_b[:], offs2)
 
-        gain_row = (0, PACK)
-
         def load_gain(s, vec):
-            nc.sync.dma_start(
-                out=gain_rows[gain_row[s] : gain_row[s] + PACK, :].rearrange("t (b i) -> t b i", i=8),
-                in_=vec.rearrange("(b t i) -> t b i", t=PACK, i=8),
-            )
+            nc.sync.dma_start(out=gain_rows[s : s + 1, :], in_=vec.unsqueeze(0))
 
         zeros_early = big.tile([P, P], F32, name="zeros_early", offset=tab_at - 2 * P)
         nc.gpsimd.memset(zeros_early[:], 0.0)
-        nc.gpsimd.tensor_copy(gain_rows[:], zeros_early[:])
+        nc.gpsimd.tensor_copy(
+            gain_rows[:].rearrange("p (t n) -> p t n", t=PACK), zeros_early[:].unsqueeze(1).to_broadcast([P, PACK, P])
+        )
         zeros_late = big.tile([P, P], F32, name="zeros_late", offset=wb_at - 2 * P)
         nc.vector.memset(zeros_late[:], 0.0)
 
@@ -110,10 +108,10 @@ def tile_list_biaff_tanh_none_kernel(
             nc.sync.dma_start(out=tab[a][:], in_=tab_words[a].rearrange("p t i -> p (t i)").bitcast(I32))
 
         load_words(wa_raw[:, 0:W_WORDS], wa_words)
-        load_table(0)
-        nc.gpsimd.memset(raw_plane[0], 0)
         load_gain(0, sa)
         load_gain(1, sb)
+        load_table(0)
+        nc.gpsimd.memset(raw_plane[0], 0)
         load_plane(raw_plane[0], wa_scales)
         load_table(1)
         nc.gpsimd.memset(raw_plane[1], 0)
@@ -195,12 +193,16 @@ def tile_list_biaff_tanh_none_kernel(
                     nc.scalar.activation(th[:, h, :, :], sums[(i, h)][:].rearrange("p t n -> p n t"), ACT.Tanh)
                 tanh_tiles[i] = th
 
-        gains = const_psum.tile([P, P], F32, name="gains")
-        nc.tensor.transpose(gains[:], gain_rows[:], ident[:])
+        nc.gpsimd.tensor_copy(
+            gain_by_place[:].rearrange("p t (b i) -> p t b i", i=8), gain_rows[:].rearrange("p (b t i) -> p t b i", t=PACK, i=8)
+        )
+        gains = const_psum.tile([P, PACK, P], F32, name="gains")
+        for t in range(PACK):
+            nc.tensor.transpose(gains[:, t, :], gain_by_place[:, t, :], ident[:])
         gains_a = held.tile([P, BLOCK, PACK], F32, name="gains_a")
-        nc.scalar.copy(gains_a[:], gains[:, gain_row[0] : gain_row[0] + PACK].unsqueeze(1).to_broadcast([P, BLOCK, PACK]))
+        nc.scalar.copy(gains_a[:], gains[:, :, 0].unsqueeze(1).to_broadcast([P, BLOCK, PACK]))
         gains_b = held.tile([P, PACK], F32, name="gains_b")
-        nc.scalar.copy(gains_b[:], gains[:, gain_row[1] : gain_row[1] + PACK])
+        nc.scalar.copy(gains_b[:], gains[:, :, 1])
         hb16 = [ring.tile([P, CHUNK, PACK], BF16, name="hb16", align_bytes=64) for c in range(2)]
 
         first_stage(0, 0)
@@ -246,7 +248,7 @@ def tile_list_biaff_tanh_none_kernel(
             nc.vector.tensor_tensor(
                 out=h16[:].rearrange("p n (u e) -> p n u e", e=2),
                 in0=th.rearrange("p u n e -> p n u e"),
-                in1=gains[:, gain_row[1] : gain_row[1] + PACK]
+                in1=gains[:, :, 1]
                 .rearrange("p (u e) -> p u e", e=2)
                 .unsqueeze(1)
                 .to_broadcast([P, width, 2, 2]),

@@ -65,7 +65,7 @@ def tile_list_biaff_tanh_none_kernel(
 
         tab_at = 4 * W_RAW
         wb_at = tab_at + PASSES * 4 * T
-        nc.vector.memset(tab_plane[:].bitcast(I32), 0)
+        nc.gpsimd.memset(tab_plane[:].bitcast(I32), 0)
         nc.sync.dma_start(list_a[:], offs)
         load_plane(tab_plane[:].bitcast(I32), tab_scales, (0, 2))
         for a in range(PASSES):
@@ -79,18 +79,14 @@ def tile_list_biaff_tanh_none_kernel(
         def load_gain(s, vec):
             nc.sync.dma_start(out=gain_rows[s : s + 1, :], in_=vec.unsqueeze(0))
 
-        zeros_early = big.tile([P, P], F32, name="zeros_early", offset=tab_at - 2 * P)
-        nc.gpsimd.memset(zeros_early[:], 0.0)
-        nc.gpsimd.tensor_copy(
-            gain_rows[:].rearrange("p (t n) -> p t n", t=PACK), zeros_early[:].unsqueeze(1).to_broadcast([P, PACK, P])
-        )
-        zeros_late = big.tile([P, P], F32, name="zeros_late", offset=wb_at - 2 * P)
-        nc.vector.memset(zeros_late[:], 0.0)
+        nc.gpsimd.memset(gain_rows[:], 0.0)
+        zeros = held.tile([P, P], F32, name="zeros")
+        nc.vector.memset(zeros[:], 0.0)
 
         ident = held.tile([P, P], F32, name="ident")
         nc.gpsimd.affine_select(
             out=ident[:],
-            in_=zeros_late[:],
+            in_=zeros[:],
             compare_op=mybir.AluOpType.not_equal,
             fill=1.0,
             base=0,
@@ -99,9 +95,10 @@ def tile_list_biaff_tanh_none_kernel(
         )
 
         wa_raw = big.tile([P, W_RAW], I32, name="wa_raw", offset=0, align_bytes=64)
-        wb_raw = big.tile([P, W_RAW], I32, name="wb_raw", offset=wb_at, align_bytes=64)
+        wb_raw = big.tile([P, W_WORDS], I32, name="wb_raw", offset=wb_at, align_bytes=64)
         raw_words = ((wa_raw[:, 0:R], wa_raw[:, R:W_WORDS]), (wb_raw[:, 0:R], wb_raw[:, R:W_WORDS]))
-        raw_plane = (wa_raw[:, W_WORDS:W_RAW], wb_raw[:, W_WORDS:W_RAW])
+        wb_raw_plane = tanhs.tile([P, R // 4], I32, name="wb_raw_plane", offset=4 * PACK * CHUNK - R // 2, align_bytes=64)
+        raw_plane = (wa_raw[:, W_WORDS:W_RAW], wb_raw_plane[:])
         tab = [big.tile([P, T], I32, name="tab%d" % a, offset=tab_at + a * 4 * T, align_bytes=64) for a in range(PASSES)]
 
         def load_table(a):
@@ -125,17 +122,20 @@ def tile_list_biaff_tanh_none_kernel(
         for s in range(2):
             nc.vector.tensor_copy(picked_plane[s][:], tab_plane[:].indirect(lists[s][:]))
 
+        def move_plane(s, copy):
+            copy(
+                w_plane[s][:].bitcast(U32).rearrange("p (t b i) -> p t b i", t=PACK, i=2),
+                raw_plane[s].bitcast(U32).rearrange("p (b t i) -> p t b i", t=PACK, i=2),
+            )
+
         for s in range(2):
             for a in range(PASSES):
                 nc.gpsimd.tensor_copy(
                     out=w_codes[s][a][:].bitcast(I32).rearrange("p (t b i) -> p t b i", t=PACK, i=8),
                     in_=raw_words[s][a].rearrange("p (b t i) -> p t b i", t=PACK, i=8),
                 )
-                if a == 0:
-                    nc.gpsimd.tensor_copy(
-                        out=w_plane[s][:].bitcast(I32).rearrange("p (t b i) -> p t b i", t=PACK, i=2),
-                        in_=raw_plane[s].rearrange("p (b t i) -> p t b i", t=PACK, i=2),
-                    )
+                if (s, a) == (0, 0):
+                    move_plane(0, nc.gpsimd.tensor_copy)
 
         chunks = [(0, c) for c in range(M // CHUNK)] + [(1, c) for c in range(J // CHUNK)]
         picked = {}
@@ -143,9 +143,12 @@ def tile_list_biaff_tanh_none_kernel(
         def gather_words(i, a, slot):
             s, c = chunks[i]
             words = picks.tile([P, CHUNK], U32, name="picked%d%d" % (i, a), offset=4 * CHUNK * slot, align_bytes=64)
-            nc.vector.tensor_copy(
-                words[:], tab[a][:].bitcast(U32).indirect(lists[s][:, c * CHUNK // 16 : (c + 1) * CHUNK // 16])
-            )
+            piece = BLOCK if (i, a) == (0, 1) else CHUNK
+            for first in range(0, CHUNK, piece):
+                at = c * CHUNK + first
+                nc.vector.tensor_copy(
+                    words[:, first : first + piece], tab[a][:].bitcast(U32).indirect(lists[s][:, at // 16 : (at + piece) // 16])
+                )
             picked[(i, a)] = words
 
         for a in range(PASSES):
@@ -203,6 +206,7 @@ def tile_list_biaff_tanh_none_kernel(
         nc.scalar.copy(gains_a[:], gains[:, :, 0].unsqueeze(1).to_broadcast([P, BLOCK, PACK]))
         gains_b = held.tile([P, PACK], F32, name="gains_b")
         nc.scalar.copy(gains_b[:], gains[:, :, 1])
+        move_plane(1, nc.scalar.copy)
         hb16 = [ring.tile([P, CHUNK, PACK], BF16, name="hb16", align_bytes=64) for c in range(2)]
 
         first_stage(0, 0)

@@ -95,10 +95,10 @@ def tile_list_biaff_tanh_none_kernel(
         )
 
         wa_raw = big.tile([P, W_RAW], I32, name="wa_raw", offset=0, align_bytes=64)
-        wb_raw = big.tile([P, W_WORDS], I32, name="wb_raw", offset=wb_at, align_bytes=64)
-        raw_words = ((wa_raw[:, 0:R], wa_raw[:, R:W_WORDS]), (wb_raw[:, 0:R], wb_raw[:, R:W_WORDS]))
-        wb_raw_plane = tanhs.tile([P, R // 4], I32, name="wb_raw_plane", offset=4 * PACK * CHUNK - R // 2, align_bytes=64)
-        raw_plane = (wa_raw[:, W_WORDS:W_RAW], wb_raw_plane[:])
+        wb_first = tanhs.tile([P, R + R // 4], I32, name="wb_first", offset=4 * PACK * CHUNK - R // 2, align_bytes=64)
+        wb_second = big.tile([P, R], I32, name="wb_second", offset=wb_at + 2 * R, align_bytes=64)
+        raw_words = ((wa_raw[:, 0:R], wa_raw[:, R:W_WORDS]), (wb_first[:, 0:R], wb_second[:]))
+        raw_plane = (wa_raw[:, W_WORDS:W_RAW], wb_first[:, R : R + R // 4])
         tab = [big.tile([P, T], I32, name="tab%d" % a, offset=tab_at + a * 4 * T, align_bytes=64) for a in range(PASSES)]
 
         def load_table(a):
@@ -128,14 +128,17 @@ def tile_list_biaff_tanh_none_kernel(
                 raw_plane[s].bitcast(U32).rearrange("p (b t i) -> p t b i", t=PACK, i=2),
             )
 
-        for s in range(2):
-            for a in range(PASSES):
-                nc.gpsimd.tensor_copy(
-                    out=w_codes[s][a][:].bitcast(I32).rearrange("p (t b i) -> p t b i", t=PACK, i=8),
-                    in_=raw_words[s][a].rearrange("p (b t i) -> p t b i", t=PACK, i=8),
-                )
-                if (s, a) == (0, 0):
-                    move_plane(0, nc.gpsimd.tensor_copy)
+        def move_words(s, a, first, last, copy):
+            copy(
+                w_codes[s][a][:].rearrange("p (t b i) -> p t b i", t=PACK, i=8)[:, :, first // 32 : last // 32],
+                raw_words[s][a][:, first:last].bitcast(U32).rearrange("p (b t i) -> p t b i", t=PACK, i=8),
+            )
+
+        move_words(0, 0, 0, R, nc.gpsimd.tensor_copy)
+        move_plane(0, nc.gpsimd.tensor_copy)
+        move_words(0, 1, 0, R, nc.gpsimd.tensor_copy)
+        move_words(1, 0, R // 2, R, nc.gpsimd.tensor_copy)
+        move_words(1, 1, 0, R, nc.gpsimd.tensor_copy)
 
         chunks = [(0, c) for c in range(M // CHUNK)] + [(1, c) for c in range(J // CHUNK)]
         picked = {}
@@ -207,6 +210,7 @@ def tile_list_biaff_tanh_none_kernel(
         gains_b = held.tile([P, PACK], F32, name="gains_b")
         nc.scalar.copy(gains_b[:], gains[:, :, 1])
         move_plane(1, nc.scalar.copy)
+        move_words(1, 0, 0, R // 2, nc.scalar.copy)
         hb16 = [ring.tile([P, CHUNK, PACK], BF16, name="hb16", align_bytes=64) for c in range(2)]
 
         first_stage(0, 0)

from contextlib import ExitStack

import concourse.mybir as mybir

K, R, T, M, J = 1024, 512, 2048, 512, 1024
FLOPS = 2 * K * R * (M + J) + 2 * R * M * J

F32 = mybir.dt.float32
BF16 = mybir.dt.bfloat16
I32 = mybir.dt.int32
U32 = mybir.dt.uint32
U16 = mybir.dt.uint16
U8 = mybir.dt.uint8
FP8X4 = mybir.dt.float8_e4m3fn_x4
ACT = mybir.ActivationFunctionType
MULT = mybir.AluOpType.mult

P = 128
PASSES = 2
PACK = 4
BLOCK = 128
CHUNK = 256
OUT_SCALE = 0.03125
W_WORDS = PASSES * R
W_RAW = W_WORDS + R // 4
AHEAD = 4
ON_SCALAR = 48
EARLY = 160


def tile_list_biaff_tanh_none_kernel(
    tc, tab_words, tab_scales, wa_words, wa_scales, wb_words, wb_scales, sa, sb, offs, offs2, out
):
    nc = tc.nc
    with ExitStack() as ctx:
        held = ctx.enter_context(tc.tile_pool(name="held", bufs=1))
        big = ctx.enter_context(tc.tile_pool(name="big", bufs=1))
        picks = ctx.enter_context(tc.tile_pool(name="picks", bufs=1))
        ring = ctx.enter_context(tc.tile_pool(name="ring", bufs=4))
        tanhs = ctx.enter_context(tc.tile_pool(name="tanhs", bufs=1))
        wide = ctx.enter_context(tc.tile_pool(name="wide", bufs=10))
        const_psum = ctx.enter_context(tc.psum_pool(name="const_psum", bufs=1))
        banks = ctx.enter_context(tc.psum_pool(name="banks", bufs=7))

        list_a = held.tile([P, M // 16], U16, name="list_a")
        list_b = held.tile([P, J // 16], U16, name="list_b")
        lists = (list_a, list_b)
        tab_plane = held.tile([P, T], U8, name="tab_plane", align_bytes=64)
        w_plane = [held.tile([P, R], U8, name="w_plane%d" % s, align_bytes=64) for s in range(2)]
        w_codes = [
            [held.tile([P, R], U32, name="w_codes%d%d" % (s, a), align_bytes=64) for a in range(PASSES)]
            for s in range(2)
        ]
        gain_rows = held.tile([P, R], F32, name="gain_rows")
        gain_by_place = held.tile([P, PACK, P], F32, name="gain_by_place")

        def load_plane(plane, scales, quadrants=range(4)):
            for q in quadrants:
                nc.sync.dma_start(out=plane[32 * q : 32 * q + 8, :], in_=scales[:, 4 * q : 4 * q + 4, :].bitcast(I32))

        def load_words(raw, words):
            nc.sync.dma_start(
                out=raw.rearrange("p (a r) -> p a r", a=PASSES), in_=words.rearrange("a p r i -> p a (r i)").bitcast(I32)
            )

        tab_at = 4 * W_RAW
        wb_at = tab_at + PASSES * 4 * T
        nc.gpsimd.memset(tab_plane[:].bitcast(I32), 0)
        nc.sync.dma_start(list_a[:], offs)
        load_plane(tab_plane[:].bitcast(I32), tab_scales, (0, 2))
        for a in range(PASSES):
            for q in (1, 3):
                nc.sync.dma_start(
                    out=tab_plane[:].bitcast(I32)[32 * q + 4 * a : 32 * q + 4 * a + 4, :],
                    in_=tab_scales[a, 4 * q : 4 * q + 4, :].bitcast(I32),
                )
        nc.sync.dma_start(list_b[:], offs2)

        def load_gain(s, vec):
            nc.sync.dma_start(out=gain_rows[s : s + 1, :], in_=vec.unsqueeze(0))

        nc.gpsimd.memset(gain_rows[:], 0.0)
        zeros = held.tile([P, P], F32, name="zeros")
        nc.vector.memset(zeros[:], 0.0)

        ident = held.tile([P, P], F32, name="ident")
        nc.gpsimd.affine_select(
            out=ident[:],
            in_=zeros[:],
            compare_op=mybir.AluOpType.not_equal,
            fill=1.0,
            base=0,
            pattern=[[-1, P]],
            channel_multiplier=1,
        )

        wa_raw = big.tile([P, W_RAW], I32, name="wa_raw", offset=0, align_bytes=64)
        wb_first = tanhs.tile([P, R + R // 4], I32, name="wb_first", offset=4 * PACK * CHUNK - R // 2, align_bytes=64)
        wb_second = big.tile([P, R], I32, name="wb_second", offset=wb_at + 2 * R, align_bytes=64)
        raw_words = ((wa_raw[:, 0:R], wa_raw[:, R:W_WORDS]), (wb_first[:, 0:R], wb_second[:]))
        raw_plane = (wa_raw[:, W_WORDS:W_RAW], wb_first[:, R : R + R // 4])
        tab = [big.tile([P, T], I32, name="tab%d" % a, offset=tab_at + a * 4 * T, align_bytes=64) for a in range(PASSES)]

        def load_table(a):
            nc.sync.dma_start(out=tab[a][:], in_=tab_words[a].rearrange("p t i -> p (t i)").bitcast(I32))

        load_words(wa_raw[:, 0:W_WORDS], wa_words)
        load_gain(0, sa)
        load_gain(1, sb)
        load_table(0)
        nc.gpsimd.memset(raw_plane[0], 0)
        load_plane(raw_plane[0], wa_scales)
        load_table(1)
        nc.gpsimd.memset(raw_plane[1], 0)
        load_plane(raw_plane[1], wb_scales)
        for a in range(PASSES):
            nc.sync.dma_start(out=raw_words[1][a], in_=wb_words[a].rearrange("p r i -> p (r i)").bitcast(I32))

        picked_plane = [
            held.tile([P, n], U8, name="picked_plane%d" % s, align_bytes=64) for s, n in enumerate((M, J))
        ]
        for s in range(2):
            nc.vector.tensor_copy(picked_plane[s][:], tab_plane[:].indirect(lists[s][:]))

        def move_plane(s, copy):
            copy(
                w_plane[s][:].bitcast(U32).rearrange("p (t b i) -> p t b i", t=PACK, i=2),
                raw_plane[s].bitcast(U32).rearrange("p (b t i) -> p t b i", t=PACK, i=2),
            )

        def move_words(s, a, first, last, copy):
            copy(
                w_codes[s][a][:].rearrange("p (t b i) -> p t b i", t=PACK, i=8)[:, :, first // 32 : last // 32],
                raw_words[s][a][:, first:last].bitcast(U32).rearrange("p (b t i) -> p t b i", t=PACK, i=8),
            )

        move_words(0, 0, 0, R, nc.gpsimd.tensor_copy)
        move_plane(0, nc.gpsimd.tensor_copy)
        move_words(0, 1, 0, R, nc.gpsimd.tensor_copy)
        move_words(1, 0, R // 2, R, nc.gpsimd.tensor_copy)
        move_words(1, 1, 0, R, nc.gpsimd.tensor_copy)

        chunks = [(0, c) for c in range(M // CHUNK)] + [(1, c) for c in range(J // CHUNK)]
        picked = {}

        def gather_words(i, a, slot):
            s, c = chunks[i]
            words = picks.tile([P, CHUNK], U32, name="picked%d%d" % (i, a), offset=4 * CHUNK * slot, align_bytes=64)
            piece = BLOCK if (i, a) == (0, 1) else CHUNK
            for first in range(0, CHUNK, piece):
                at = c * CHUNK + first
                nc.vector.tensor_copy(
                    words[:, first : first + piece], tab[a][:].bitcast(U32).indirect(lists[s][:, at // 16 : (at + piece) // 16])
                )
            picked[(i, a)] = words

        for a in range(PASSES):
            for i in range(AHEAD):
                gather_words(i, a, a * AHEAD + i)
        freed = [AHEAD] + [a * AHEAD + i for i in range(1, AHEAD) for a in range(PASSES)][1:]
        for n, (i, a) in enumerate([(i, a) for i in range(AHEAD, len(chunks)) for a in range(PASSES)]):
            gather_words(i, a, freed[n])

        tanh_tiles = {}
        split_chunk = M // CHUNK + 1
        sums = {}

        def first_stage(i, a):
            s, c = chunks[i]
            width = BLOCK if s == 0 else CHUNK
            places = PACK * BLOCK // width
            for h in range(2):
                if a == 0:
                    sums[(i, h)] = banks.tile([P, places, width], F32, name="bank")
                first = h * BLOCK if s == 0 else 0
                for n in range(places):
                    t = n if s == 0 else h * places + n
                    nc.tensor.matmul_mx(
                        out=sums[(i, h)][:, n, :],
                        lhsT=w_codes[s][a][:, t * P : (t + 1) * P].bitcast(FP8X4),
                        lhsT_scale=w_plane[s][4 * a :, t * P : (t + 1) * P],
                        rhs=picked[(i, a)][:, first : first + width].bitcast(FP8X4),
                        rhs_scale=picked_plane[s][4 * a :, c * CHUNK + first : c * CHUNK + first + width],
                        start=(a == 0 and n == 0),
                        stop=(a == PASSES - 1 and n == places - 1),
                    )
            if a == PASSES - 1 and i == split_chunk:
                at = i * 4 * PACK * CHUNK
                early = tanhs.tile([P, 2, EARLY, 2], F32, name="th_early", offset=at, align_bytes=64)
                rest = tanhs.tile([P, 2, CHUNK - EARLY, 2], F32, name="th_rest", offset=at + 4 * PACK * EARLY, align_bytes=64)
                for h in range(2):
                    nc.scalar.activation(early[:, h, :, :], sums[(i, h)][:, :, :EARLY].rearrange("p t n -> p n t"), ACT.Tanh)
                    nc.scalar.activation(rest[:, h, :, :], sums[(i, h)][:, :, EARLY:].rearrange("p t n -> p n t"), ACT.Tanh)
                tanh_tiles[i] = early
                tanh_tiles["rest"] = rest
            elif a == PASSES - 1:
                th = tanhs.tile([P, 2, width, places], F32, name="th%d" % i, offset=i * 4 * PACK * CHUNK, align_bytes=64)
                for h in range(2):
                    nc.scalar.activation(th[:, h, :, :], sums[(i, h)][:].rearrange("p t n -> p n t"), ACT.Tanh)
                tanh_tiles[i] = th

        nc.gpsimd.tensor_copy(
            gain_by_place[:].rearrange("p t (b i) -> p t b i", i=8), gain_rows[:].rearrange("p (b t i) -> p t b i", t=PACK, i=8)
        )
        gains = const_psum.tile([P, PACK, P], F32, name="gains")
        for t in range(PACK):
            nc.tensor.transpose(gains[:, t, :], gain_by_place[:, t, :], ident[:])
        gains_a = held.tile([P, BLOCK, PACK], F32, name="gains_a")
        nc.scalar.copy(gains_a[:], gains[:, :, 0].unsqueeze(1).to_broadcast([P, BLOCK, PACK]))
        gains_b = held.tile([P, PACK], F32, name="gains_b")
        nc.scalar.copy(gains_b[:], gains[:, :, 1])
        move_plane(1, nc.scalar.copy)
        move_words(1, 0, 0, R // 2, nc.scalar.copy)
        hb16 = [ring.tile([P, CHUNK, PACK], BF16, name="hb16", align_bytes=64) for c in range(2)]

        first_stage(0, 0)
        first_stage(1, 0)
        first_stage(0, 1)
        first_stage(1, 1)
        for i in range(M // CHUNK, len(chunks)):
            for a in range(PASSES):
                first_stage(i, a)
            if i == M // CHUNK + 1:
                by_place = held.tile([P, PACK, ON_SCALAR], BF16, name="by_place", align_bytes=64)
                for t in range(PACK):
                    nc.scalar.activation(
                        by_place[:, t, :], tanh_tiles[i][:, t // 2, 0:ON_SCALAR, t % 2], ACT.Copy, scale=gains_b[:, t : t + 1]
                    )
                nc.scalar.copy(hb16[1][:, 0:ON_SCALAR, :], by_place[:].rearrange("p t n -> p n t"))

        th_bytes = 4 * PACK * CHUNK
        h16_bytes = 2 * PACK * CHUNK

        def quantise(h16, codes, plane):
            nc.vector.quantize_mx(out=codes.bitcast(FP8X4), scales=plane, in_=h16.rearrange("p n t -> p (n t)"))

        ha16 = []
        for c in range(M // CHUNK):
            h16 = big.tile([P, CHUNK, PACK], BF16, name="ha16_%d" % c, offset=wb_at + c * h16_bytes, align_bytes=64)
            step = c + 1
            for h in range(0, CHUNK // BLOCK, step):
                nc.gpsimd.tensor_tensor(
                    out=h16[:, h * BLOCK : (h + step) * BLOCK, :].rearrange("p (h n) t -> p h (n t)", h=step),
                    in0=tanh_tiles[c][:, h : h + step, :, :].rearrange("p h n t -> p h (n t)"),
                    in1=gains_a[:].rearrange("p n t -> p (n t)").unsqueeze(1).to_broadcast([P, step, BLOCK * PACK]),
                    op=MULT,
                )
            ha16.append(h16)

        def scale_b(col, h16):
            width = h16.shape[1]
            if col == CHUNK + EARLY:
                th = tanh_tiles["rest"][:]
            else:
                th = tanh_tiles[M // CHUNK + col // CHUNK][:, :, col % CHUNK : col % CHUNK + width, :]
            nc.vector.tensor_tensor(
                out=h16[:].rearrange("p n (u e) -> p n u e", e=2),
                in0=th.rearrange("p u n e -> p n u e"),
                in1=gains[:, :, 1]
                .rearrange("p (u e) -> p u e", e=2)
                .unsqueeze(1)
                .to_broadcast([P, width, 2, 2]),
                op=MULT,
            )
            return h16

        out_view = out.rearrange("(u p) j -> p u j", p=P)

        first_codes = tanhs.tile([P, M + J // 2], U32, name="first_codes", offset=split_chunk * th_bytes - th_bytes // 2, align_bytes=64)
        first_plane = held.tile([P, M + J // 2], U8, name="first_plane", align_bytes=64)

        def scores(row_tiles, codes, plane, res, on_vector=False):
            y = banks.tile([P, len(row_tiles), codes.shape[1]], F32, name="bank")
            for n, u in enumerate(row_tiles):
                nc.tensor.matmul_mx(
                    out=y[:, n, :],
                    lhsT=first_codes[:, u * P : (u + 1) * P].bitcast(FP8X4),
                    lhsT_scale=first_plane[:, u * P : (u + 1) * P],
                    rhs=codes.bitcast(FP8X4),
                    rhs_scale=plane,
                    start=True,
                    stop=True,
                )
            if on_vector:
                nc.vector.tensor_scalar_mul(res, y[:], OUT_SCALE)
            else:
                nc.scalar.activation(res, y[:], ACT.Copy, scale=OUT_SCALE)

        def store(row_tiles, col, res):
            nc.sync.dma_start(out=out_view[:, row_tiles[0] : row_tiles[-1] + 1, col : col + res.shape[2]], in_=res)

        def quantise_first(h16, at):
            quantise(h16, first_codes[:, at : at + h16.shape[1]], first_plane[:, at : at + h16.shape[1]])

        def first_scores(row_tiles, col, width):
            res = wide.tile([P, len(row_tiles), width], F32, name="res")
            cols = slice(M + col, M + col + width)
            scores(row_tiles, first_codes[:, cols], first_plane[:, cols], res[:])
            store(row_tiles, col, res[:])

        scale_b(0, hb16[0])
        scale_b(CHUNK + ON_SCALAR, hb16[1][:, ON_SCALAR:EARLY, :])
        scale_b(CHUNK + EARLY, hb16[1][:, EARLY:, :])
        quantise_first(ha16[0][:, 0:BLOCK, :], 0)
        quantise_first(hb16[0][:], M)
        first_scores((0,), 0, CHUNK)
        quantise_first(ha16[0][:, BLOCK:CHUNK, :], BLOCK)
        first_scores((1,), 0, CHUNK)
        quantise_first(hb16[1][:], M + CHUNK)
        first_scores((0, 1), CHUNK, CHUNK)
        quantise_first(ha16[1][:], CHUNK)
        first_scores((2,), 0, 2 * CHUNK)
        first_scores((3,), 0, 2 * CHUNK)

        late16 = big.tile([P, J // 2, PACK], BF16, name="late16", offset=wb_at - h16_bytes, align_bytes=64)
        halves = ((0, 1), (2, 3))
        for c in (2, 3):
            res = [wide.tile([P, 2, CHUNK], F32, name="res") for half in halves]
            blocks = []
            for first in range(0, CHUNK, BLOCK):
                col = c * CHUNK + first
                h16 = scale_b(col, late16[:, col - J // 2 : col - J // 2 + BLOCK, :])
                codes = ring.tile([P, BLOCK], U32, name="hb_codes", align_bytes=64)
                plane = ring.tile([P, BLOCK], U8, name="hb_plane", align_bytes=64)
                quantise(h16, codes[:], plane[:])
                blocks.append((first, codes, plane))
            order = [(n, k) for n in range(2) for k in range(2)] if c == 2 else [(n, k) for k in range(2) for n in range(2)]
            for n, k in order:
                first, codes, plane = blocks[k]
                scores(halves[n], codes[:], plane[:], res[n][:, :, first : first + BLOCK], on_vector=(c == 3 and n == 1))
                if k == 1:
                    store(halves[n], c * CHUNK, res[n][:])
